import numpy as np, ml_dtypes
CORES = [6,15,38,47]
N = 4
import mx_ref
BF = ml_dtypes.bfloat16
def pick(q, e):
    c = np.concatenate([q[0].reshape(128, -1, 4), np.zeros((128, 1, 4), np.uint8)], axis=1); s = np.concatenate([q[1], np.ones((16, 1), np.uint8)], axis=1)
    return (np.ascontiguousarray(c[:, e].reshape(128, -1)), np.ascontiguousarray(s[:, e]))
def join(*qs):
    return (np.concatenate([q[0] for q in qs], axis=1), np.concatenate([q[1] for q in qs], axis=1))
def put(q, e, v):
    c, s = q[0].reshape(128, -1, 4).copy(), q[1].copy(); c[:, e] = v[0].reshape(128, -1, 4); s[:, e] = v[1]
    return (c.reshape(128, -1), s)
def pk(c, s):
    return (np.ascontiguousarray(c), mx_ref.live(s))
def emit(q):
    return q[0], q[1]
def decode(q):
    o = []
    for b in range(4):
        e = np.zeros((128, 128, 4), np.float32); e[np.arange(128), np.arange(128), b] = 1
        o.append(mx_ref.matmul(mx_ref.quantize(e.reshape(128, 512).astype(BF)), q))
    return np.stack(o, axis=2).reshape(128, -1)
def f(rng, *shape):
    return mx_ref.flush((rng.standard_normal(shape, dtype=np.float32) * np.exp2(rng.integers(-2, 3, shape[:-1] + (1,)))).astype(BF))
def wide(rng, *shape, cols=0):
    v = rng.standard_normal(shape, dtype=np.float32) * np.exp2(rng.integers(-12, 13, shape)).astype(np.float32)
    if cols: v *= np.repeat(np.exp2(rng.integers(-cols, cols + 1, shape[:-2] + (1, shape[-1] // 4))) * (rng.random(shape[:-2] + (1, shape[-1] // 4)) > 0.0625), 4, axis=-1).astype(np.float32)
    return mx_ref.flush(v.astype(BF))
P, C, G, H = 96, 160, 16, 3
F = 96
def trim(v):
    v = v.astype(np.float32)
    v[np.abs(v) < np.float32(2.0 ** -20)] = 0
    return v.astype(BF)
def alike(v):
    return np.stack([v] * N).astype(np.float32).astype(BF)
def flat(v):
    return v.reshape(N, 128, -1).astype(np.float32).astype(BF)
def planted(rng, sign, m, a, b):
    v, t = 1 + rng.random((N, 128, P, 4)), 1 + rng.random((N, 128, C, 4))
    if sign < 0:
        v = 64.0 * (1 + (np.argsort(v, axis=-1) < 2))
        t[:] = 4
    for r in range(N):
        if sign < 0: v[r, m[r], np.arange(P)] = 128
        else: v[r, m[r], np.arange(P)] *= 64
        at = rng.permutation(np.arange(C) % F)
        g = np.zeros(C)
        if sign > 0:
            g[:] = 4
            o = rng.permutation(C)
            g[o[np.unique(at[o], return_index=True)[1]]] = 16
        t[r, at, np.arange(C)] *= g[:, None]
        t[r, :F] *= 2.0 ** 25 if sign < 0 else 2.0 ** 20
        t[r, F:] = 0
        t[r, F + 16:] = -b[r, at][None, :, None] * 2.0 ** 24
    v *= sign * 2.0 ** 20
    v[:, F:] = 0
    v[:, F:F + 16] = -a[:, None, :, None] * 2.0 ** 24
    u = np.zeros((128, 4))
    u[F:] = 2.0 ** 29
    return {"pn": flat(v), "x": flat(t), "u": alike(u), "w": f(rng, N, 128, 512)}
def setup_inputs(rng):
    return {"pn": trim(f(rng, N, 128, 4 * P)), "x": trim(f(rng, N, 128, 4 * C)), "u": alike(f(rng, 128, 4)), "w": f(rng, N, 128, 512)}
def setup_inputs_near(rng):
    K = min(P, C // 2)
    z = rng.integers(4, 8, (128, K, 4)) * rng.choice([-1.0, 1.0], (128, K, 4))
    z[:16] = 0
    u = rng.integers(4, 8, (128, 4)) * rng.choice([-1.0, 1.0], (128, 4))
    u[:16] = 0
    u[8, 0] = 2.0 ** -8
    v, t = np.zeros((N, 128, P, 4)), np.zeros((N, 128, C, 4))
    for r in range(N):
        v[r] = z[:, rng.permutation(np.arange(P) % K)]
        v[r, 0, :, 0] = 2.0 ** -4
        at = rng.permutation(np.arange(C) % K)
        small = np.ones(C)
        for k in range(K):
            e = np.flatnonzero(at == k)
            if k % 3 == 0: small[e[-1]] = 2
            if k % 3 == 2: small[e[0]] = 2
        more = np.full(K, -1.0)
        o = rng.permutation(K)
        more[o[:K // 2]] = 1
        more[o[K // 2:K // 2 + K // 4]] = 0
        t[r] = z[:, at]
        t[r, 0, :, 0] = small * 2.0 ** -4
        t[r, 8, :, 0] = more[at] * 2.0 ** -4
    g = 2.0 ** -int(rng.integers(12, 17))
    return {"pn": flat(v * g), "x": flat(t * g), "u": alike(u * 2.0 ** -int(rng.integers(12, 21))), "w": f(rng, N, 128, 512)}
def setup_inputs_below(rng):
    m, b = np.stack([rng.permutation(F)[:P] for r in range(N)]), np.full((N, F), 4.0)
    for r in range(N): b[(r + 1) % N, m[r, rng.permutation(P)[:2 * G]]] = 1
    return planted(rng, -1, m, np.full((N, P), 2.0), b)
def setup_inputs_crowd(rng):
    E = P // 2
    n = rng.permutation(np.array([G, 0, G + 1, G - 1, 1, E, G, G + 1])[:N])
    m, a = np.zeros((N, P), int), np.full((N, P), 8.0)
    for r in range(N):
        g = rng.permutation(np.arange(P) % E)
        m[r] = rng.permutation(F)[g]
        a[r, np.unique(g, return_index=True)[1][rng.permutation(E)[n[r]:]]] = 2
    return planted(rng, 1, m, a, np.full((N, F), 4.0))
def setup_inputs_spread(rng):
    return {**setup_inputs(rng), "pn": trim(wide(rng, N, 128, 4 * P, cols=6)), "x": trim(wide(rng, N, 128, 4 * C, cols=6))}
def check_inputs(d):
    b = []
    for k, lo, hi in (("pn", -20, 27), ("x", -20, 27), ("u", -30, 30), ("w", -30, 30)):
        v = np.abs(d[k].astype(np.float32))
        if not (np.isfinite(v).all() and ((v == 0) | (v >= 2.0 ** lo) & (v <= 2.0 ** hi)).all()): b.append("a value of " + k)
    v = d["u"].astype(np.float32)
    if not (v == v[:1]).all(): b.append("u differs between ranks")
    return b
def upto(e, n):
    return np.concatenate([e, np.full(n - len(e), -1)])
def visit(a, b, k):
    s = mx_ref.matmul(pick(a, upto(np.arange(P), 128)), b)[:P] + np.float32(0)
    place = np.argmax(s, axis=1)
    v = mx_ref.matmul(k, join(a, b))[0] + np.float32(0)
    owns = np.zeros(P, bool)
    owns[np.unique(place, return_index=True)[1]] = True
    i = np.flatnonzero(owns & (v[P + place] > v[:P]))[:G]
    if len(i) == 0: return a, b
    j = place[i]
    d = decode(join(pick(a, upto(i, G)), pick(b, upto(j, G))))
    z = mx_ref.quantize(np.ascontiguousarray((d[:, :4 * G] - np.float32(0.5) * d[:, 4 * G:]).astype(BF)))
    return put(a, i, pick(b, j)), put(b, j, pick(z, np.arange(len(i))))
def reference(pn, x, u, w):
    a = [mx_ref.quantize(np.ascontiguousarray(pn[r])) for r in range(N)]
    b = [mx_ref.quantize(np.ascontiguousarray(x[r])) for r in range(N)]
    k = [mx_ref.quantize(np.concatenate([u[r], np.zeros((128, 508), BF)], axis=1)) for r in range(N)]
    wq = [mx_ref.quantize(np.ascontiguousarray(w[r])) for r in range(N)]
    y = np.zeros((N, 128, H * P), np.float32)
    for h in range(H):
        a = [a[r - 1] for r in range(N)]
        for r in range(N):
            a[r], b[r] = visit(a[r], b[r], k[r])
            y[r, :, h * P:h * P + P] = mx_ref.matmul(wq[r], a[r])
    p, t = [emit(v) for v in a], [emit(v) for v in b]
    return {"y": y, "pc": np.stack([v[0] for v in p]), "psc": np.stack([v[1] for v in p]), "oc": np.stack([v[0] for v in t]), "osc": np.stack([v[1] for v in t])}

@@ -1,0 +1,275 @@
+from concourse.mybir import dt, AluOpType, AxisListType, ActivationFunctionType
+
+P, C, G, H = 96, 160, 16, 3
+X4, U8, BF, F32, U16, I32 = "float8_e4m3fn_x4", "uint8", "bfloat16", "float32", "uint16", "int32"
+BIG = 1e29
+
+SCRATCH = {}
+
+
+def _mx(name, n):
+    SCRATCH[name + "c"] = ("sbuf", [128, n], X4)
+    SCRATCH[name + "s"] = ("sbuf", [128, n], U8)
+
+
+_mx("p0", 128)
+for _h in range(1, H + 1):
+    _mx("q%d" % _h, 384)
+    _mx("p%d" % _h, 224)
+    SCRATCH["off%d" % _h] = ("sbuf", [128, 8], U16)
+    SCRATCH["oft%d" % _h] = ("sbuf", [128, 16], U16)
+_mx("ot", C)
+_mx("eq", 1024)
+_mx("kq", 256)
+_mx("uq", 288)
+_mx("wq", 128)
+_mx("c1", C)
+_mx("c2", 128)
+for _n, _w, _d in (("pt", 512, BF), ("xt", 640, BF), ("wt", 512, BF), ("ul", 8, BF), ("ut", 1152, BF), ("zero", 512, BF),
+                   ("eb", 1040, BF), ("kt", 1024, BF), ("dd", 128, BF), ("m16", 128, BF), ("ta", 128, BF), ("tb", 128, BF),
+                   ("tl", 128, BF), ("pi", 4, I32), ("pf", 4, F32), ("j6", 8, F32), ("gor", 16, F32), ("gof", 16, F32),
+                   ("go", 16, U16), ("sv", P, F32), ("tw", 768, F32), ("mk", 48, F32), ("sc", 18, F32), ("t1", 640, BF),
+                   ("t2", 512, BF), ("zt", 512, BF), ("pm", 176, F32), ("sm", 4, F32), ("mn", 4, F32), ("jk", 16, F32),
+                   ("l18", 18, F32), ("tg", C, F32), ("tt", C, F32), ("ys", H * P, F32)):
+    SCRATCH[_n] = ("sbuf", [128, _w], _d)
+for _b in range(8):
+    SCRATCH["ps%d" % _b] = ("psum", [128, 512], F32)
+
+SEMAPHORES = ["arr1", "arr2", "arr3", "sent", "ldP", "ldU", "ldX", "ldW", "gA", "gM", "gB", "gC", "z", "i1", "i2", "i3", "i4",
+              "i5", "a1", "a2", "ut", "qP", "eqP", "eqN", "uq", "kq", "wq", "sS", "sPen", "sM1", "sM2", "z0", "z1", "z2", "z3",
+              "sY", "vS", "t1", "q1", "pad", "vR", "t2", "q2", "vL", "off", "pc", "ps", "sc", "zc", "zq", "tg", "vT", "oft",
+              "tbC", "tbS", "aA", "aB", "yc", "out"]
+
+
+def rank_program(g, core, T, topo):
+    rank = T.rank_of(core)
+    if rank is None:
+        return
+    A, AF = AluOpType, ActivationFunctionType
+    v, a, pe, sy, S = g.vector, g.scalar, g.tensor, g.sync, T.sem
+    nxt = T.cores[(rank + 1) % len(T.cores)]
+    rid, pid, _ = topo.addr(nxt)
+    mask, ne = topo.mask(core, nxt), len(topo.engines(core, nxt))
+
+    def quant(name, lo, hi, tile):
+        return v.quantize_mx(T[name + "c"][:, lo:hi], T[name + "s"][:, lo:hi], tile)
+
+    def mm(bank, w, wlo, x, lo, hi, start=True, stop=True):
+        return pe.matmul_mx(T["ps%d" % bank][:, 0:hi - lo], T[w + "c"][:, wlo:wlo + 128], T[w + "s"][:, wlo:wlo + 128],
+                            T[x + "c"][:, lo:hi], T[x + "s"][:, lo:hi], start, stop)
+
+    def send(h, part):
+        src, dst = T["p%d%s" % (h, part)][:, 0:P], T["q%d%s" % (h + 1, part)][:, 0:P]
+        if part == "c":
+            src, dst = src.bitcast(dt.uint8), dst.bitcast(dt.uint8)
+        g.remote_dma(dst, src, S["arr%d" % (h + 1)], S.sent, pid, rid, mask)
+
+    def pick_codes(dst, dlo, dhi, src, lo, hi, off):
+        return v.tensor_copy(T[dst + "c"][:, dlo:dhi].bitcast(dt.uint32), T[src + "c"][:, lo:hi].bitcast(dt.uint32).indirect(off))
+
+    def pick_scales(dst, dlo, dhi, src, lo, hi, off):
+        return a.activation(T[dst + "s"][:, dlo:dhi], T[src + "s"][:, lo:hi].indirect(off), AF.Copy)
+
+    sy.dma_start(T.pt[:, 0:4 * P], T.pn[:]).then_inc(S.ldP, 16)
+    sy.dma_start(T.ul[:, 0:4], T.u[:]).then_inc(S.ldU, 16)
+    sy.dma_start(T.xt[:], T.x[:]).then_inc(S.ldX, 16)
+    sy.dma_start(T.wt[:], T.w[:]).then_inc(S.ldW, 16)
+    sy.wait_ge(S.yc, H - 1)
+    sy.wait_ge(S["arr%d" % H], 2 * ne)
+    sy.dma_start(T.y[:, 0:(H - 1) * P], T.ys[:, 0:(H - 1) * P]).then_inc(S.out, 16)
+    sy.wait_ge(S.pc, H)
+    sy.dma_start(T.pc[:], T["p%dc" % H][:, 0:P].bitcast(dt.uint8)).then_inc(S.out, 16)
+    sy.wait_ge(S.ps, H)
+    for k in range(4):
+        sy.dma_start(T.psc[4 * k:4 * k + 4, :], T["p%ds" % H][32 * k:32 * k + 4, 0:P]).then_inc(S.out, 16)
+    sy.wait_ge(S.yc, H)
+    sy.dma_start(T.y[:, (H - 1) * P:H * P], T.ys[:, (H - 1) * P:H * P]).then_inc(S.out, 16)
+    sy.wait_ge(S.tbC, H + 1)
+    sy.dma_start(T.oc[:], T.otc[:].bitcast(dt.uint8)).then_inc(S.out, 16)
+    sy.wait_ge(S.tbS, H)
+    for k in range(2):
+        sy.dma_start(T.osc[4 * k:4 * k + 4, :], T.ots[32 * k:32 * k + 4, :]).then_inc(S.out, 16)
+    sy.wait_ge(S.out, 16 * 12)
+
+    fl = {"allow_small_or_imprecise_dtypes": True}
+    g.iota(T.dd[:], [[1, 128]], 0, -1, **fl).then_inc(S.gA, 1)
+    g.iota(T.pi[:, 0:1], [[1, 1]], 0, 1).then_inc(S.gA, 1)
+    g.iota(T.m16[:], [[0, 8], [1, 16]], 0, 0, **fl).then_inc(S.gM, 1)
+    g.wait_ge(S.qP, 1)
+    send(0, "c")
+    send(0, "s")
+    g.iota(T.j6[:], [[1, 8]], 0, 0, **fl).then_inc(S.gB, 1)
+    g.iota(T.gor[:, 0:10], [[32, 5], [0, 2]], 0, 0, **fl).then_inc(S.gB, 1)
+    g.iota(T.sv[:], [[1, P]], C, 0, **fl).then_inc(S.gC, 1)
+    g.iota(T.tw[:], [[0, H], [1, 256]], -P, 0, **fl).then_inc(S.gC, 1)
+    for h in range(1, H):
+        g.wait_ge(S.pc, h)
+        send(h, "c")
+        g.wait_ge(S.ps, h)
+        send(h, "s")
+    g.wait_ge(S.sent, 2 * ne * H)
+
+    a.wait_ge(S.z, 1)
+    fills = ((T.t1[:, 3:640:4], 160, 0.0), (T.t2[:], 512, 0.0), (T.kt[:, 3:512:4], 128, 0.0), (T.kt[:, 514:1024:4], 128, -1.0),
+             (T.zt[:, 384:512], 128, 0.0), (T.pm[:, 0:1], 1, -BIG), (T.mk[:], 48, 0.0), (T.sc[:, 0:18:3], 6, 1000.0),
+             (T.sc[:, 1:18:3], 6, 0.0))
+    for out, n, c in fills:
+        a.activation(out, T.zero[:, 0:n], AF.Identity, bias=c).then_inc(S.a1, 1)
+    a.wait_ge(S.ldU, 16)
+    for t in range(4):
+        a.activation(T.ut[:, t:640:4], T.zero[:, 0:160], AF.Identity, bias=T.ul[:, t:t + 1]).then_inc(S.a2, 1)
+    a.wait_ge(S.a2, 4)
+    a.activation(T.ut[:, 640:1152], T.ut[:, 0:512], AF.Identity, scale=-1.0).then_inc(S.ut, 1)
+
+    v.memset(T.zero[:], 0.0).then_inc(S.z, 1)
+    v.memset(T.pt[:, 4 * P:512], 0.0).then_inc(S.i1, 1)
+    v.memset(T.eb[:], 0.0).then_inc(S.i1, 1)
+    v.wait_ge(S.i1, 2)
+    v.wait_ge(S.gA, 2)
+    v.tensor_scalar(T.pi[:, 1:2], T.pi[:, 0:1], 15, None, A.bitwise_and).then_inc(S.i2, 1)
+    v.tensor_scalar(T.pi[:, 2:3], T.pi[:, 0:1], 31, None, A.bitwise_and).then_inc(S.i2, 1)
+    v.tensor_scalar(T.pi[:, 3:4], T.pi[:, 0:1], 4, None, A.arith_shift_right).then_inc(S.i2, 1)
+    v.tensor_scalar(T.eb[:, 3:515:4], T.dd[:], 0.0, None, A.is_equal).then_inc(S.i2, 1)
+    v.tensor_scalar(T.eb[:, 523:1035:4], T.dd[:], 0.0, -0.5, A.is_equal, A.mult).then_inc(S.i2, 1)
+    v.tensor_scalar(T.kt[:, 2:512:4], T.dd[:], 0.0, None, A.is_equal).then_inc(S.i2, 1)
+    v.tensor_scalar(T.ta[:], T.dd[:], 0.0, 4.0, A.is_gt, A.mult).then_inc(S.i2, 1)
+    v.tensor_scalar(T.tb[:], T.dd[:], 0.0, 2.0, A.is_equal, A.mult).then_inc(S.i2, 1)
+    v.wait_ge(S.ldP, 16)
+    quant("p0", 0, 128, T.pt[:]).then_inc(S.qP, 1)
+    v.wait_ge(S.i2, 8)
+    v.tensor_copy(T.pf[:, 0:3], T.pi[:, 1:4]).then_inc(S.i3, 1)
+    v.tensor_tensor(T.kt[:, 0:512:4], T.ta[:], T.tb[:], A.subtract).then_inc(S.i3, 1)
+    v.tensor_tensor(T.kt[:, 1:512:4], T.tb[:], T.ta[:], A.subtract).then_inc(S.i3, 1)
+    for b in range(4):
+        quant("eq", 128 * b, 128 * b + 128, T.eb[:, 3 - b:515 - b]).then_inc(S.eqP, 1)
+    v.wait_ge(S.ldX, 16)
+    quant("q1", P, P + C, T.xt[:]).then_inc(S.tbC, 1)
+    v.wait_ge(S.i3, 3)
+    v.wait_ge(S.gM, 1)
+    v.wait_ge(S.gB, 2)
+    v.wait_ge(S.a1, len(fills))
+    pr, p32, pc = T.pf[:, 0:1], T.pf[:, 1:2], T.pf[:, 2:3]
+    v.tensor_scalar(T.kt[:, 513:1024:4], T.m16[:], pr, float(G), A.is_equal, A.mult).then_inc(S.i4, 1)
+    v.tensor_scalar(T.kt[:, 515:1024:4], T.m16[:], pr, None, A.is_equal).then_inc(S.i4, 1)
+    v.tensor_scalar(T.tl[:], T.m16[:], pr, None, A.is_gt).then_inc(S.i4, 1)
+    v.tensor_scalar(T.mk[:, 4:36:6], T.j6[:, 0:6], pc, 97.0, A.is_equal, A.mult).then_inc(S.i4, 1)
+    v.tensor_scalar(T.mk[:, 5:36:6], T.j6[:, 0:6], pc, 97.0, A.is_gt, A.mult).then_inc(S.i4, 1)
+    v.tensor_scalar(T.mk[:, 36:42], T.j6[:, 0:6], pc, 100.0 + P // 16, A.is_equal, A.mult).then_inc(S.i4, 1)
+    v.tensor_scalar(T.mk[:, 42:48], T.j6[:, 0:6], pc, 100.0, A.is_equal, A.mult).then_inc(S.i4, 1)
+    v.tensor_scalar(T.sc[:, 2:18:3], T.j6[:, 0:6], 16.0, pr, A.mult, A.add).then_inc(S.i4, 1)
+    v.tensor_scalar(T.gof[:, 0:10], T.gor[:, 0:10], p32, None, A.add).then_inc(S.i4, 1)
+    v.wait_ge(S.ut, 1)
+    quant("uq", 0, 288, T.ut[:]).then_inc(S.uq, 1)
+    v.wait_ge(S.i4, 9)
+    v.tensor_tensor(T.kt[:, 512:1024:4], T.kt[:, 513:1024:4], T.tl[:], A.subtract).then_inc(S.i5, 1)
+    v.tensor_scalar(T.mk[:], T.mk[:], -100.0, None, A.add).then_inc(S.i5, 1)
+    v.tensor_copy(T.go[:, 0:10], T.gof[:, 0:10]).then_inc(S.i5, 1)
+    for b in range(4):
+        quant("eq", 512 + 128 * b, 640 + 128 * b, T.eb[:, 523 - b:1035 - b]).then_inc(S.eqN, 1)
+    v.wait_ge(S.i5, 3)
+    quant("kq", 0, 256, T.kt[:]).then_inc(S.kq, 1)
+    v.wait_ge(S.ldW, 16)
+    quant("wq", 0, 128, T.wt[:]).then_inc(S.wq, 1)
+
+    for h in range(1, H + 1):
+        q, p = "q%d" % h, "p%d" % h
+        off, oft = T["off%d" % h][:, 0:P // 16], T["oft%d" % h][:, 0:C // 16]
+        tdst, tlo = ("q%d" % (h + 1), P) if h < H else ("ot", 0)
+        tw0 = 256 * (h - 1)
+        top = T.pm[:, C:C + 1]
+
+        pe.wait_ge(S.tbC, h)
+        if h == 1:
+            pe.wait_ge(S.uq, 1)
+        else:
+            pe.wait_ge(S.tbS, h - 1)
+        mm(1, "uq", C, q, P, P + C, True, False)
+        pe.wait_ge(S["arr%d" % h], 2 * ne)
+        mm(0, q, 0, q, P, P + C).then_inc(S.sS, 1)
+        mm(1, q, 0, "uq", 0, C, False, True).then_inc(S.sPen, 1)
+        if h == 1:
+            pe.wait_ge(S.eqP, 4)
+        for b in range(4):
+            mm(4 + b, "eq", 128 * b, q, 0, 128, True, False)
+        if h == 1:
+            pe.wait_ge(S.kq, 1)
+        else:
+            pe.wait_ge(S.yc, h - 1)
+        pe.wait_ge(S.q1, h)
+        mm(2, "kq", 0, "c1", 0, C).then_inc(S.sM1, 1)
+        pe.wait_ge(S.q2, h)
+        mm(3, "kq", 128, "c2", 0, 128).then_inc(S.sM2, 1)
+        if h == 1:
+            pe.wait_ge(S.eqN, 4)
+            pe.wait_ge(S.wq, 1)
+        pe.wait_ge(S.pad, h)
+        pe.wait_ge(S.pc, h)
+        pe.wait_ge(S.ps, h)
+        for b in range(4):
+            mm(4 + b, "eq", 512 + 128 * b, p, 0, 128, False, True).then_inc(S["z%d" % b], 1)
+        mm(2, "wq", 0, p, 0, 128).then_inc(S.sY, 1)
+
+        a.wait_ge(S.sPen, h)
+        a.activation(T.t1[:, 2:640:4], T.ps1[:, 0:C], AF.Sign).then_inc(S.t1, 1)
+        a.wait_ge(S.vS, h)
+        a.activation(T.t1[:, 1:640:4], T.pm[:, 1:C + 1], AF.Sign, bias=top, scale=-1.0, accum_out=T.sm[:, 0:1]).then_inc(S.t1, 1)
+        a.activation(T.jk[:, 0:10], T.pm[:, 16:C + 1:16], AF.Sign, bias=top, scale=-1.0, accum_out=T.sm[:, 1:2]).then_inc(S.aA, 1)
+        if h == 1:
+            a.wait_ge(S.i5, 3)
+        a.wait_ge(S.t1, 3 * h)
+        a.wait_ge(S.aA, h)
+        a.activation(T.sm[:, 2:3], T.sm[:, 1:2], AF.Identity, bias=T.sm[:, 0:1], scale=-16.0).then_inc(S.aB, 1)
+        a.activation(T.t2[:, 5:72:12], T.mk[:, 36:42], AF.Relu, bias=T.sm[:, 1:2]).then_inc(S.t2, 1)
+        a.wait_ge(S.aB, h)
+        a.activation(T.t2[:, 7:72:12], T.mk[:, 42:48], AF.Relu, bias=T.sm[:, 2:3]).then_inc(S.t2, 1)
+        a.wait_ge(S.off, h)
+        pick_scales(p, 0, P, q, 0, 256, off).then_inc(S.ps, 1)
+        for b in range(2):
+            a.wait_ge(S["z%d" % b], h)
+            a.activation(T.zt[:, b:384:4], T["ps%d" % (4 + b)][:, 0:P], AF.Copy).then_inc(S.zc, 1)
+        a.wait_ge(S.sc, h)
+        a.activation(T.tg[:], T.tw[:, tw0 + P:tw0 + 256].indirect(T.go[:, 0:10]), AF.Copy).then_inc(S.tg, 1)
+        a.wait_ge(S.sY, h)
+        a.activation(T.ys[:, (h - 1) * P:h * P], T.ps2[:, 0:P], AF.Copy).then_inc(S.yc, 1)
+        a.wait_ge(S.zq, h)
+        a.wait_ge(S.oft, h)
+        pick_scales(tdst, tlo, tlo + C, q, P, 384, oft).then_inc(S.tbS, 1)
+
+        v.wait_ge(S.sS, h)
+        v.tensor_tensor_scan(T.pm[:, 1:C + 1], T.ps0[:, 0:C], T.zero[:, 0:C], -BIG, A.max, A.add).then_inc(S.vS, 1)
+        v.wait_ge(S.vS, h)
+        v.tensor_scalar(T.t1[:, 0:640:4], T.pm[:, 0:C], top, None, A.is_lt).then_inc(S.t1, 1)
+        v.wait_ge(S.t1, 3 * h)
+        quant("c1", 0, C, T.t1[:]).then_inc(S.q1, 1)
+        quant(p, P, P + 128, T.zero[:]).then_inc(S.pad, 1)
+        v.wait_ge(S.sM1, h)
+        v.tensor_reduce(T.mn[:, 0:1], T.ps2[:, 0:C], AxisListType.X, A.min).then_inc(S.vR, 1)
+        v.wait_ge(S.vR, h)
+        v.tensor_scalar(T.t2[:, 0:72:2], T.mk[:, 0:36], T.mn[:, 0:1], 256.0, A.is_equal, A.mult).then_inc(S.t2, 1)
+        v.wait_ge(S.t2, 3 * h)
+        quant("c2", 0, 128, T.t2[:]).then_inc(S.q2, 1)
+        v.wait_ge(S.sM2, h)
+        v.tensor_tensor_scan(T.l18[:], T.ps3[:, 0:18], T.sc[:], 0.0, A.min, A.max).then_inc(S.vL, 1)
+        v.wait_ge(S.vL, h)
+        v.tensor_copy(off, T.l18[:, 2:18:3]).then_inc(S.off, 1)
+        v.wait_ge(S.off, h)
+        pick_codes(p, 0, P, q, 0, 256, off).then_inc(S.pc, 1)
+        if h == 1:
+            v.wait_ge(S.gC, 2)
+        v.tensor_copy(T.tw[:, tw0:tw0 + 256].indirect(off), T.sv[:]).then_inc(S.sc, 1)
+        for b in range(2, 4):
+            v.wait_ge(S["z%d" % b], h)
+            v.tensor_copy(T.zt[:, b:384:4], T["ps%d" % (4 + b)][:, 0:P]).then_inc(S.zc, 1)
+        v.wait_ge(S.zc, 4 * h)
+        quant(q, 256, 384, T.zt[:]).then_inc(S.zq, 1)
+        v.wait_ge(S.tg, h)
+        v.transpose(T.tt[:], T.tg[:]).then_inc(S.vT, 1)
+        v.wait_ge(S.vT, h)
+        v.tensor_copy(oft, T.tt[:, 0:C:16]).then_inc(S.oft, 1)
+        v.wait_ge(S.zq, h)
+        v.wait_ge(S.oft, h)
+        pick_codes(tdst, tlo, tlo + C, q, P, 384, oft).then_inc(S.tbC, 1)
+
+    a.wait_ge(S.tbS, H)
+    for k in range(2, 4):
+        a.dma_start(T.osc[4 * k:4 * k + 4, :], T.ots[32 * k:32 * k + 4, :]).then_inc(S.out, 16)

@@ -3,6 +3,8 @@ from concourse.mybir import dt, AluOpType, AxisListType, ActivationFunctionType
 P, C, G, H = 96, 160, 16, 3
 X4, U8, BF, F32, U16, I32 = "float8_e4m3fn_x4", "uint8", "bfloat16", "float32", "uint16", "int32"
 BIG = 1e29
+NG = P // 16
+CW = C + 8 * NG
 
 SCRATCH = {}
 
@@ -23,22 +25,23 @@ _mx("eq", 1024)
 _mx("kq", 256)
 _mx("uq", 288)
 _mx("wq", 128)
-_mx("c1", C)
+_mx("c1", CW)
 _mx("c2", 128)
+_mx("c3", 128)
 for _n, _w, _d in (("pt", 512, BF), ("xt", 640, BF), ("wt", 512, BF), ("ul", 8, BF), ("ut", 1152, BF), ("zero", 512, BF),
-                   ("eb", 1040, BF), ("kt", 1024, BF), ("dd", 128, BF), ("m16", 128, BF), ("ta", 128, BF), ("tb", 128, BF),
-                   ("tl", 128, BF), ("pi", 4, I32), ("pf", 4, F32), ("j6", 8, F32), ("gor", 16, F32), ("gof", 16, F32),
-                   ("go", 16, U16), ("sv", P, F32), ("tw", 768, F32), ("mk", 48, F32), ("sc", 18, F32), ("t1", 640, BF),
-                   ("t2", 512, BF), ("zt", 512, BF), ("pm", 176, F32), ("sm", 4, F32), ("mn", 4, F32), ("jk", 16, F32),
-                   ("l18", 18, F32), ("tg", C, F32), ("tt", C, F32), ("ys", H * P, F32)):
+                   ("eb", 520, BF), ("en", 520, BF), ("kt", 1024, BF), ("dd", 128, BF), ("m16", C, BF), ("ta", 128, BF),
+                   ("tb", 128, BF), ("pi", 4, I32), ("pf", 8, F32), ("j48", 48, F32), ("sv", P, F32), ("tw", 768, F32),
+                   ("mk", 24, F32), ("m1", CW, F32), ("sc", 12, F32), ("s1", 64 + 4 * CW, BF), ("s2", C + 512, BF),
+                   ("s3", 512, BF), ("zt", 512, BF), ("pm", 192, F32), ("sm", 4, F32), ("jk", 16, F32), ("ls", 12, F32),
+                   ("hm", C, BF), ("hq", 16, F32), ("hc", 4, F32), ("tt", C, F32), ("ys", H * P, F32)):
     SCRATCH[_n] = ("sbuf", [128, _w], _d)
 for _b in range(8):
     SCRATCH["ps%d" % _b] = ("psum", [128, 512], F32)
 
-SEMAPHORES = ["arr1", "arr2", "arr3", "sent", "ldP", "ldU", "ldX", "ldW", "gA", "gM", "gB", "gC", "z", "i1", "i2", "i3", "i4",
-              "i5", "a1", "a2", "ut", "qP", "eqP", "eqN", "uq", "kq", "wq", "sS", "sPen", "sM1", "sM2", "z0", "z1", "z2", "z3",
-              "sY", "vS", "t1", "q1", "pad", "vR", "t2", "q2", "vL", "off", "pc", "ps", "sc", "zc", "zq", "tg", "vT", "oft",
-              "tbC", "tbS", "aA", "aB", "yc", "out"]
+SEMAPHORES = ["arr1", "arr2", "arr3", "sent", "ldP", "ldU", "ldX", "ldW", "gA", "gM", "gB", "gC", "z", "i0", "i1", "i2", "i3",
+              "i4", "i5", "i6", "i7", "i8", "ed", "a1", "a2", "a3", "a4", "ut", "en", "qP", "eqP", "eqN", "uq", "kq", "wq", "sS",
+              "sPen", "sM1", "sM2", "sM3", "z0", "z1", "z2", "z3", "sY", "vS", "t1", "q1", "pad", "t2", "q2", "t3", "q3", "ld",
+              "vL", "off", "pc", "ps", "sc", "zc", "zq", "vT", "oft", "tbC", "tbS", "aA", "yc", "out"]
 
 
 def rank_program(g, core, T, topo):
@@ -49,7 +52,8 @@ def rank_program(g, core, T, topo):
     v, a, pe, sy, S = g.vector, g.scalar, g.tensor, g.sync, T.sem
     nxt = T.cores[(rank + 1) % len(T.cores)]
     rid, pid, _ = topo.addr(nxt)
-    mask, ne = topo.mask(core, nxt), len(topo.engines(core, nxt))
+    es = topo.engines(core, nxt)
+    ne = len(es)
 
     def quant(name, lo, hi, tile):
         return v.quantize_mx(T[name + "c"][:, lo:hi], T[name + "s"][:, lo:hi], tile)
@@ -58,17 +62,17 @@ def rank_program(g, core, T, topo):
         return pe.matmul_mx(T["ps%d" % bank][:, 0:hi - lo], T[w + "c"][:, wlo:wlo + 128], T[w + "s"][:, wlo:wlo + 128],
                             T[x + "c"][:, lo:hi], T[x + "s"][:, lo:hi], start, stop)
 
-    def send(h, part):
+    def send(h, part, engines):
         src, dst = T["p%d%s" % (h, part)][:, 0:P], T["q%d%s" % (h + 1, part)][:, 0:P]
         if part == "c":
             src, dst = src.bitcast(dt.uint8), dst.bitcast(dt.uint8)
-        g.remote_dma(dst, src, S["arr%d" % (h + 1)], S.sent, pid, rid, mask)
+        g.remote_dma(dst, src, S["arr%d" % (h + 1)], S.sent, pid, rid, sum(1 << e for e in engines))
 
-    def pick_codes(dst, dlo, dhi, src, lo, hi, off):
-        return v.tensor_copy(T[dst + "c"][:, dlo:dhi].bitcast(dt.uint32), T[src + "c"][:, lo:hi].bitcast(dt.uint32).indirect(off))
+    def pick_codes(dst, dlo, dhi, src, hi, off):
+        return v.tensor_copy(T[dst + "c"][:, dlo:dhi].bitcast(dt.uint32), T[src + "c"][:, 0:hi].bitcast(dt.uint32).indirect(off))
 
-    def pick_scales(dst, dlo, dhi, src, lo, hi, off):
-        return a.activation(T[dst + "s"][:, dlo:dhi], T[src + "s"][:, lo:hi].indirect(off), AF.Copy)
+    def pick_scales(dst, dlo, dhi, src, hi, off):
+        return a.activation(T[dst + "s"][:, dlo:dhi], T[src + "s"][:, 0:hi].indirect(off), AF.Copy)
 
     sy.dma_start(T.pt[:, 0:4 * P], T.pn[:]).then_inc(S.ldP, 16)
     sy.dma_start(T.ul[:, 0:4], T.u[:]).then_inc(S.ldU, 16)
@@ -93,26 +97,27 @@ def rank_program(g, core, T, topo):
 
     fl = {"allow_small_or_imprecise_dtypes": True}
     g.iota(T.dd[:], [[1, 128]], 0, -1, **fl).then_inc(S.gA, 1)
-    g.iota(T.pi[:, 0:1], [[1, 1]], 0, 1).then_inc(S.gA, 1)
-    g.iota(T.m16[:], [[0, 8], [1, 16]], 0, 0, **fl).then_inc(S.gM, 1)
+    g.iota(T.pi[:, 0:1], [[1, 1]], 0, 1).then_inc(S.gM, 1)
+    g.iota(T.m16[:], [[0, C // 16], [1, 16]], 0, 0, **fl).then_inc(S.gM, 1)
     g.wait_ge(S.qP, 1)
-    send(0, "c")
-    send(0, "s")
-    g.iota(T.j6[:], [[1, 8]], 0, 0, **fl).then_inc(S.gB, 1)
-    g.iota(T.gor[:, 0:10], [[32, 5], [0, 2]], 0, 0, **fl).then_inc(S.gB, 1)
-    g.iota(T.sv[:], [[1, P]], C, 0, **fl).then_inc(S.gC, 1)
-    g.iota(T.tw[:], [[0, H], [1, 256]], -P, 0, **fl).then_inc(S.gC, 1)
+    send(0, "c", es[:ne // 2])
+    send(0, "s", es[ne // 2:])
+    g.iota(T.j48[:], [[-1, 8 * NG]], 8 * NG - 1, 0, **fl).then_inc(S.gB, 1)
+    g.iota(T.sv[:], [[1, P]], P + C, 0, **fl).then_inc(S.gC, 1)
+    for h in range(H):
+        g.iota(T.tw[:, 256 * h + P:256 * h + 256], [[1, C]], P, 0, **fl).then_inc(S.gC, 1)
     for h in range(1, H):
         g.wait_ge(S.pc, h)
-        send(h, "c")
+        send(h, "c", es)
         g.wait_ge(S.ps, h)
-        send(h, "s")
-    g.wait_ge(S.sent, 2 * ne * H)
+        send(h, "s", es)
+    g.wait_ge(S.sent, ne * (2 * H - 1))
 
+    pr, pc = T.pf[:, 0:1], T.pf[:, 1:2]
+    j6 = T.j48[:, 0:8 * NG:8]
     a.wait_ge(S.z, 1)
-    fills = ((T.t1[:, 3:640:4], 160, 0.0), (T.t2[:], 512, 0.0), (T.kt[:, 3:512:4], 128, 0.0), (T.kt[:, 514:1024:4], 128, -1.0),
-             (T.zt[:, 384:512], 128, 0.0), (T.pm[:, 0:1], 1, -BIG), (T.mk[:], 48, 0.0), (T.sc[:, 0:18:3], 6, 1000.0),
-             (T.sc[:, 1:18:3], 6, 0.0))
+    fills = ((T.s1[:, 67:64 + 4 * C:4], C, 1.0), (T.s1[:, 64 + 4 * C:64 + 4 * CW], 4 * (CW - C), 0.0), (T.s3[:], 512, 0.0),
+             (T.zt[:, 384:512], 128, 0.0), (T.pm[:, 0:17], 17, -BIG), (T.m1[:, 0:C], C, 1000.0))
     for out, n, c in fills:
         a.activation(out, T.zero[:, 0:n], AF.Identity, bias=c).then_inc(S.a1, 1)
     a.wait_ge(S.ldU, 16)
@@ -120,63 +125,79 @@ def rank_program(g, core, T, topo):
         a.activation(T.ut[:, t:640:4], T.zero[:, 0:160], AF.Identity, bias=T.ul[:, t:t + 1]).then_inc(S.a2, 1)
     a.wait_ge(S.a2, 4)
     a.activation(T.ut[:, 640:1152], T.ut[:, 0:512], AF.Identity, scale=-1.0).then_inc(S.ut, 1)
+    a.wait_ge(S.i4, 1)
+    a.activation(T.pf[:, 2:3], pc, AF.Identity, bias=2.0, scale=8.0).then_inc(S.a4, 1)
+    a.activation(T.pf[:, 3:4], pc, AF.Identity, bias=7.0, scale=8.0).then_inc(S.a4, 1)
+    a.activation(T.pf[:, 4:5], pr, AF.Identity, bias=-14.0).then_inc(S.a4, 1)
+    a.wait_ge(S.ed, 1)
+    a.activation(T.en[:, 0:516], T.eb[:, 0:516], AF.Identity, scale=-0.5).then_inc(S.en, 1)
+    a.wait_ge(S.a4, 3)
+    a.wait_ge(S.gB, 1)
+    a.activation(T.sc[:, 1:12:2], j6, AF.Identity, bias=T.pf[:, 4:5], scale=2.0).then_inc(S.a3, 1)
+    a.wait_ge(S.i5, 1)
+    a.activation(T.hq[:], T.hm[:, 0:16], AF.Identity, bias=1.0, scale=-0.1875).then_inc(S.i7, 1)
+    a.wait_ge(S.i8, 1)
+    a.activation(T.mk[:, 8:14], T.mk[:, 0:6], AF.Identity, bias=-100.0, scale=105.0).then_inc(S.a3, 1)
+    a.activation(T.mk[:, 16:22], T.mk[:, 0:6], AF.Identity, bias=-100.0, scale=99.9375).then_inc(S.a3, 1)
+    a.wait_ge(S.a3, 3)
+    a.wait_ge(S.a1, len(fills))
 
     v.memset(T.zero[:], 0.0).then_inc(S.z, 1)
-    v.memset(T.pt[:, 4 * P:512], 0.0).then_inc(S.i1, 1)
+    v.memset(T.pt[:, 4 * P:512], 0.0).then_inc(S.i0, 1)
     v.memset(T.eb[:], 0.0).then_inc(S.i1, 1)
-    v.wait_ge(S.i1, 2)
-    v.wait_ge(S.gA, 2)
-    v.tensor_scalar(T.pi[:, 1:2], T.pi[:, 0:1], 15, None, A.bitwise_and).then_inc(S.i2, 1)
-    v.tensor_scalar(T.pi[:, 2:3], T.pi[:, 0:1], 31, None, A.bitwise_and).then_inc(S.i2, 1)
-    v.tensor_scalar(T.pi[:, 3:4], T.pi[:, 0:1], 4, None, A.arith_shift_right).then_inc(S.i2, 1)
-    v.tensor_scalar(T.eb[:, 3:515:4], T.dd[:], 0.0, None, A.is_equal).then_inc(S.i2, 1)
-    v.tensor_scalar(T.eb[:, 523:1035:4], T.dd[:], 0.0, -0.5, A.is_equal, A.mult).then_inc(S.i2, 1)
-    v.tensor_scalar(T.kt[:, 2:512:4], T.dd[:], 0.0, None, A.is_equal).then_inc(S.i2, 1)
-    v.tensor_scalar(T.ta[:], T.dd[:], 0.0, 4.0, A.is_gt, A.mult).then_inc(S.i2, 1)
-    v.tensor_scalar(T.tb[:], T.dd[:], 0.0, 2.0, A.is_equal, A.mult).then_inc(S.i2, 1)
+    v.wait_ge(S.i1, 1)
+    v.wait_ge(S.gA, 1)
+    v.tensor_scalar(T.eb[:, 3:515:4], T.dd[:], 0.0, None, A.is_equal).then_inc(S.ed, 1)
+    v.tensor_scalar(T.ta[:], T.dd[:], 0.0, -1024.0, A.is_gt, A.mult).then_inc(S.i2, 1)
+    v.wait_ge(S.i0, 1)
     v.wait_ge(S.ldP, 16)
     quant("p0", 0, 128, T.pt[:]).then_inc(S.qP, 1)
-    v.wait_ge(S.i2, 8)
-    v.tensor_copy(T.pf[:, 0:3], T.pi[:, 1:4]).then_inc(S.i3, 1)
-    v.tensor_tensor(T.kt[:, 0:512:4], T.ta[:], T.tb[:], A.subtract).then_inc(S.i3, 1)
-    v.tensor_tensor(T.kt[:, 1:512:4], T.tb[:], T.ta[:], A.subtract).then_inc(S.i3, 1)
+    v.wait_ge(S.gM, 2)
+    v.tensor_scalar(T.pi[:, 1:2], T.pi[:, 0:1], 15, None, A.bitwise_and).then_inc(S.i2, 1)
+    v.tensor_scalar(T.pi[:, 2:3], T.pi[:, 0:1], 4, None, A.arith_shift_right).then_inc(S.i2, 1)
+    v.tensor_scalar(T.tb[:], T.dd[:], 0.0, 512.0, A.is_equal, A.mult).then_inc(S.i2, 1)
+    v.tensor_scalar(T.kt[:, 2:512:4], T.dd[:], 0.0, -256.0, A.is_equal, A.mult).then_inc(S.i6, 1)
+    v.tensor_scalar(T.kt[:, 3:512:4], T.dd[:], 0.0, -512.0, A.is_equal, A.mult).then_inc(S.i6, 1)
+    v.memset(T.s2[:, CW:C + 512], 0.0).then_inc(S.i6, 1)
+    v.wait_ge(S.i2, 4)
+    v.tensor_copy(T.pf[:, 0:2], T.pi[:, 1:3]).then_inc(S.i4, 1)
+    v.tensor_tensor(T.kt[:, 0:512:4], T.ta[:], T.tb[:], A.add).then_inc(S.i3, 1)
+    v.wait_ge(S.ed, 1)
     for b in range(4):
         quant("eq", 128 * b, 128 * b + 128, T.eb[:, 3 - b:515 - b]).then_inc(S.eqP, 1)
+    v.wait_ge(S.i3, 1)
+    v.tensor_scalar(T.kt[:, 1:512:4], T.kt[:, 0:512:4], -1.0, None, A.mult).then_inc(S.i6, 1)
+    v.wait_ge(S.i4, 1)
+    v.tensor_scalar(T.hm[:], T.m16[:], pr, 4.0, A.is_gt, A.mult).then_inc(S.i5, 1)
+    for e, c, op in ((512, float(G), A.is_equal), (513, -1.0, A.is_gt), (514, -float(G), A.is_equal), (515, -1.0, A.is_le)):
+        v.tensor_scalar(T.kt[:, e:1024:4], T.m16[:, 0:128], pr, c, op, A.mult).then_inc(S.i6, 1)
     v.wait_ge(S.ldX, 16)
     quant("q1", P, P + C, T.xt[:]).then_inc(S.tbC, 1)
-    v.wait_ge(S.i3, 3)
-    v.wait_ge(S.gM, 1)
-    v.wait_ge(S.gB, 2)
-    v.wait_ge(S.a1, len(fills))
-    pr, p32, pc = T.pf[:, 0:1], T.pf[:, 1:2], T.pf[:, 2:3]
-    v.tensor_scalar(T.kt[:, 513:1024:4], T.m16[:], pr, float(G), A.is_equal, A.mult).then_inc(S.i4, 1)
-    v.tensor_scalar(T.kt[:, 515:1024:4], T.m16[:], pr, None, A.is_equal).then_inc(S.i4, 1)
-    v.tensor_scalar(T.tl[:], T.m16[:], pr, None, A.is_gt).then_inc(S.i4, 1)
-    v.tensor_scalar(T.mk[:, 4:36:6], T.j6[:, 0:6], pc, 97.0, A.is_equal, A.mult).then_inc(S.i4, 1)
-    v.tensor_scalar(T.mk[:, 5:36:6], T.j6[:, 0:6], pc, 97.0, A.is_gt, A.mult).then_inc(S.i4, 1)
-    v.tensor_scalar(T.mk[:, 36:42], T.j6[:, 0:6], pc, 100.0 + P // 16, A.is_equal, A.mult).then_inc(S.i4, 1)
-    v.tensor_scalar(T.mk[:, 42:48], T.j6[:, 0:6], pc, 100.0, A.is_equal, A.mult).then_inc(S.i4, 1)
-    v.tensor_scalar(T.sc[:, 2:18:3], T.j6[:, 0:6], 16.0, pr, A.mult, A.add).then_inc(S.i4, 1)
-    v.tensor_scalar(T.gof[:, 0:10], T.gor[:, 0:10], p32, None, A.add).then_inc(S.i4, 1)
+    v.wait_ge(S.gB, 1)
+    v.wait_ge(S.a4, 3)
+    v.tensor_scalar(T.mk[:, 0:6], j6, T.pf[:, 3:4], None, A.is_equal).then_inc(S.i8, 1)
+    v.tensor_scalar(T.m1[:, C:CW], T.j48[:], T.pf[:, 2:3], 1000.0, A.is_ge, A.mult).then_inc(S.i6, 1)
     v.wait_ge(S.ut, 1)
     quant("uq", 0, 288, T.ut[:]).then_inc(S.uq, 1)
-    v.wait_ge(S.i4, 9)
-    v.tensor_tensor(T.kt[:, 512:1024:4], T.kt[:, 513:1024:4], T.tl[:], A.subtract).then_inc(S.i5, 1)
-    v.tensor_scalar(T.mk[:], T.mk[:], -100.0, None, A.add).then_inc(S.i5, 1)
-    v.tensor_copy(T.go[:, 0:10], T.gof[:, 0:10]).then_inc(S.i5, 1)
+    v.wait_ge(S.en, 1)
     for b in range(4):
-        quant("eq", 512 + 128 * b, 640 + 128 * b, T.eb[:, 523 - b:1035 - b]).then_inc(S.eqN, 1)
-    v.wait_ge(S.i5, 3)
-    quant("kq", 0, 256, T.kt[:]).then_inc(S.kq, 1)
+        quant("eq", 512 + 128 * b, 640 + 128 * b, T.en[:, 3 - b:515 - b]).then_inc(S.eqN, 1)
+    v.wait_ge(S.i7, 1)
+    v.tensor_reduce(T.hc[:, 0:1], T.hq[:], AxisListType.X, A.mult).then_inc(S.i6, 1)
     v.wait_ge(S.ldW, 16)
     quant("wq", 0, 128, T.wt[:]).then_inc(S.wq, 1)
+    v.wait_ge(S.i6, 10)
+    v.wait_ge(S.a3, 3)
+    v.wait_ge(S.a1, len(fills))
+    quant("kq", 0, 256, T.kt[:]).then_inc(S.kq, 1)
 
     for h in range(1, H + 1):
         q, p = "q%d" % h, "p%d" % h
-        off, oft = T["off%d" % h][:, 0:P // 16], T["oft%d" % h][:, 0:C // 16]
+        off, oft = T["off%d" % h][:, 0:NG], T["oft%d" % h][:, 0:C // 16]
         tdst, tlo = ("q%d" % (h + 1), P) if h < H else ("ot", 0)
         tw0 = 256 * (h - 1)
-        top = T.pm[:, C:C + 1]
+        top = T.pm[:, 16 + C:17 + C]
+        cw = CW if h == 1 else C
 
         pe.wait_ge(S.tbC, h)
         if h == 1:
@@ -184,7 +205,7 @@ def rank_program(g, core, T, topo):
         else:
             pe.wait_ge(S.tbS, h - 1)
         mm(1, "uq", C, q, P, P + C, True, False)
-        pe.wait_ge(S["arr%d" % h], 2 * ne)
+        pe.wait_ge(S["arr%d" % h], ne if h == 1 else 2 * ne)
         mm(0, q, 0, q, P, P + C).then_inc(S.sS, 1)
         mm(1, q, 0, "uq", 0, C, False, True).then_inc(S.sPen, 1)
         if h == 1:
@@ -196,7 +217,9 @@ def rank_program(g, core, T, topo):
         else:
             pe.wait_ge(S.yc, h - 1)
         pe.wait_ge(S.q1, h)
-        mm(2, "kq", 0, "c1", 0, C).then_inc(S.sM1, 1)
+        mm(2, "kq", 0, "c1", 0, cw).then_inc(S.sM1, 1)
+        pe.wait_ge(S.q3, h)
+        mm(0, "kq", 128, "c3", 0, 128).then_inc(S.sM3, 1)
         pe.wait_ge(S.q2, h)
         mm(3, "kq", 128, "c2", 0, 128).then_inc(S.sM2, 1)
         if h == 1:
@@ -210,65 +233,60 @@ def rank_program(g, core, T, topo):
         mm(2, "wq", 0, p, 0, 128).then_inc(S.sY, 1)
 
         a.wait_ge(S.sPen, h)
-        a.activation(T.t1[:, 2:640:4], T.ps1[:, 0:C], AF.Sign).then_inc(S.t1, 1)
+        a.activation(T.s1[:, 66:64 + 4 * C:4], T.ps1[:, 0:C], AF.Sign).then_inc(S.t1, 1)
         a.wait_ge(S.vS, h)
-        a.activation(T.t1[:, 1:640:4], T.pm[:, 1:C + 1], AF.Sign, bias=top, scale=-1.0, accum_out=T.sm[:, 0:1]).then_inc(S.t1, 1)
-        a.activation(T.jk[:, 0:10], T.pm[:, 16:C + 1:16], AF.Sign, bias=top, scale=-1.0, accum_out=T.sm[:, 1:2]).then_inc(S.aA, 1)
-        if h == 1:
-            a.wait_ge(S.i5, 3)
-        a.wait_ge(S.t1, 3 * h)
+        a.activation(T.s1[:, 1:64 + 4 * C:4], T.pm[:, 1:17 + C], AF.Sign, bias=top, scale=-1.0,
+                     accum_out=T.sm[:, 0:1]).then_inc(S.t1, 1)
+        a.activation(T.jk[:, 0:12], T.pm[:, 0:17 + C:16], AF.Sign, bias=top, scale=-1.0, accum_out=T.sm[:, 1:2]).then_inc(S.aA, 1)
         a.wait_ge(S.aA, h)
-        a.activation(T.sm[:, 2:3], T.sm[:, 1:2], AF.Identity, bias=T.sm[:, 0:1], scale=-16.0).then_inc(S.aB, 1)
-        a.activation(T.t2[:, 5:72:12], T.mk[:, 36:42], AF.Relu, bias=T.sm[:, 1:2]).then_inc(S.t2, 1)
-        a.wait_ge(S.aB, h)
-        a.activation(T.t2[:, 7:72:12], T.mk[:, 42:48], AF.Relu, bias=T.sm[:, 2:3]).then_inc(S.t2, 1)
+        a.activation(T.s3[:, 0:4 * NG:4], T.mk[:, 8:14], AF.Relu, bias=T.sm[:, 1:2]).then_inc(S.t3, 1)
+        a.wait_ge(S.t1, 3 * h)
+        a.activation(T.s3[:, 2:4 * NG:4], T.mk[:, 16:22], AF.Relu, bias=T.sm[:, 1:2], scale=T.sm[:, 0:1]).then_inc(S.t3, 1)
+        a.wait_ge(S.sM3, h)
+        a.activation(T.sc[:, 0:12:2], T.ps0[:, 0:NG], AF.Copy).then_inc(S.ld, 1)
         a.wait_ge(S.off, h)
-        pick_scales(p, 0, P, q, 0, 256, off).then_inc(S.ps, 1)
-        for b in range(2):
+        pick_scales(p, 0, P, q, 256, off).then_inc(S.ps, 1)
+        for b in range(4):
             a.wait_ge(S["z%d" % b], h)
             a.activation(T.zt[:, b:384:4], T["ps%d" % (4 + b)][:, 0:P], AF.Copy).then_inc(S.zc, 1)
-        a.wait_ge(S.sc, h)
-        a.activation(T.tg[:], T.tw[:, tw0 + P:tw0 + 256].indirect(T.go[:, 0:10]), AF.Copy).then_inc(S.tg, 1)
         a.wait_ge(S.sY, h)
         a.activation(T.ys[:, (h - 1) * P:h * P], T.ps2[:, 0:P], AF.Copy).then_inc(S.yc, 1)
         a.wait_ge(S.zq, h)
         a.wait_ge(S.oft, h)
-        pick_scales(tdst, tlo, tlo + C, q, P, 384, oft).then_inc(S.tbS, 1)
+        pick_scales(tdst, tlo, tlo + C, q, 384, oft).then_inc(S.tbS, 1)
 
         v.wait_ge(S.sS, h)
-        v.tensor_tensor_scan(T.pm[:, 1:C + 1], T.ps0[:, 0:C], T.zero[:, 0:C], -BIG, A.max, A.add).then_inc(S.vS, 1)
+        v.tensor_tensor_scan(T.pm[:, 17:17 + C], T.ps0[:, 0:C], T.zero[:, 0:C], -BIG, A.max, A.add).then_inc(S.vS, 1)
         v.wait_ge(S.vS, h)
-        v.tensor_scalar(T.t1[:, 0:640:4], T.pm[:, 0:C], top, None, A.is_lt).then_inc(S.t1, 1)
+        v.tensor_scalar(T.s1[:, 64:64 + 4 * C:4], T.pm[:, 16:16 + C], top, None, A.is_lt).then_inc(S.t1, 1)
         v.wait_ge(S.t1, 3 * h)
-        quant("c1", 0, C, T.t1[:]).then_inc(S.q1, 1)
-        quant(p, P, P + 128, T.zero[:]).then_inc(S.pad, 1)
+        quant("c1", 0, cw, T.s1[:, 64:64 + 4 * cw]).then_inc(S.q1, 1)
+        v.wait_ge(S.t3, 2 * h)
+        quant("c3", 0, 128, T.s3[:]).then_inc(S.q3, 1)
         v.wait_ge(S.sM1, h)
-        v.tensor_reduce(T.mn[:, 0:1], T.ps2[:, 0:C], AxisListType.X, A.min).then_inc(S.vR, 1)
-        v.wait_ge(S.vR, h)
-        v.tensor_scalar(T.t2[:, 0:72:2], T.mk[:, 0:36], T.mn[:, 0:1], 256.0, A.is_equal, A.mult).then_inc(S.t2, 1)
-        v.wait_ge(S.t2, 3 * h)
-        quant("c2", 0, 128, T.t2[:]).then_inc(S.q2, 1)
+        v.tensor_tensor_scan(T.s2[:, 0:CW], T.ps2[:, 0:CW], T.m1[:], 0.0, A.max, A.min).then_inc(S.t2, 1)
+        v.wait_ge(S.t2, h)
+        quant("c2", 0, 128, T.s2[:, C:C + 512]).then_inc(S.q2, 1)
+        quant(p, P, P + 128, T.zero[:]).then_inc(S.pad, 1)
+        v.wait_ge(S.ld, h)
         v.wait_ge(S.sM2, h)
-        v.tensor_tensor_scan(T.l18[:], T.ps3[:, 0:18], T.sc[:], 0.0, A.min, A.max).then_inc(S.vL, 1)
+        v.tensor_tensor_scan(T.ls[:], T.ps3[:, 0:12], T.sc[:], 0.0, A.min, A.max).then_inc(S.vL, 1)
         v.wait_ge(S.vL, h)
-        v.tensor_copy(off, T.l18[:, 2:18:3]).then_inc(S.off, 1)
+        v.tensor_copy(off, T.ls[:, 11::-2]).then_inc(S.off, 1)
         v.wait_ge(S.off, h)
-        pick_codes(p, 0, P, q, 0, 256, off).then_inc(S.pc, 1)
+        pick_codes(p, 0, P, q, 256, off).then_inc(S.pc, 1)
         if h == 1:
-            v.wait_ge(S.gC, 2)
+            v.wait_ge(S.gC, 1 + H)
         v.tensor_copy(T.tw[:, tw0:tw0 + 256].indirect(off), T.sv[:]).then_inc(S.sc, 1)
-        for b in range(2, 4):
-            v.wait_ge(S["z%d" % b], h)
-            v.tensor_copy(T.zt[:, b:384:4], T["ps%d" % (4 + b)][:, 0:P]).then_inc(S.zc, 1)
+        v.wait_ge(S.sc, h)
+        v.tensor_tensor_scan(T.tt[:], T.hm[:], T.tw[:, tw0 + P:tw0 + 256], 0.0, A.mult, A.max).then_inc(S.vT, 1)
+        v.wait_ge(S.vT, h)
+        v.tensor_scalar(oft, T.tt[:, 15:C:16], T.hc[:, 0:1], None, A.mult).then_inc(S.oft, 1)
         v.wait_ge(S.zc, 4 * h)
         quant(q, 256, 384, T.zt[:]).then_inc(S.zq, 1)
-        v.wait_ge(S.tg, h)
-        v.transpose(T.tt[:], T.tg[:]).then_inc(S.vT, 1)
-        v.wait_ge(S.vT, h)
-        v.tensor_copy(oft, T.tt[:, 0:C:16]).then_inc(S.oft, 1)
         v.wait_ge(S.zq, h)
         v.wait_ge(S.oft, h)
-        pick_codes(tdst, tlo, tlo + C, q, P, 384, oft).then_inc(S.tbC, 1)
+        pick_codes(tdst, tlo, tlo + C, q, 384, oft).then_inc(S.tbC, 1)
 
     a.wait_ge(S.tbS, H)
     for k in range(2, 4):

@@ -4,6 +4,7 @@ P, C, G, H = 96, 160, 16, 3
 X4, U8, BF, F32, U16, I32 = "float8_e4m3fn_x4", "uint8", "bfloat16", "float32", "uint16", "int32"
 BIG = 1e29
 NG = P // 16
+NP = C // 16
 CW = C + 8 * NG
 
 SCRATCH = {}
@@ -17,31 +18,38 @@ def _mx(name, n):
 _mx("p0", 128)
 for _h in range(1, H + 1):
     _mx("q%d" % _h, 384)
-    _mx("p%d" % _h, 224)
     SCRATCH["off%d" % _h] = ("sbuf", [128, 8], U16)
+    SCRATCH["nm%d" % _h] = ("sbuf", [128, 8], U16)
     SCRATCH["oft%d" % _h] = ("sbuf", [128, 16], U16)
+SCRATCH["ofb"] = ("sbuf", [128, 8], U16)
+SCRATCH["lr"] = ("sbuf", [128, 8], U16)
+_mx("p2", P)
+_mx("p3", P)
+_mx("r", 2 * P)
 _mx("ot", C)
+_mx("na", 224)
+_mx("nb", 224)
 _mx("eq", 1024)
-_mx("kq", 256)
+_mx("kq", 384)
 _mx("uq", 288)
-_mx("wq", 128)
+for _n in ("wq", "c2", "c3", "c4", "lq"):
+    _mx(_n, 128)
 _mx("c1", CW)
-_mx("c2", 128)
-_mx("c3", 128)
 for _n, _w, _d in (("pt", 512, BF), ("xt", 640, BF), ("wt", 512, BF), ("ul", 8, BF), ("ut", 1152, BF), ("zero", 512, BF),
-                   ("eb", 520, BF), ("en", 520, BF), ("kt", 1024, BF), ("dd", 128, BF), ("m16", C, BF), ("ta", 128, BF),
-                   ("tb", 128, BF), ("pi", 4, I32), ("pf", 8, F32), ("j48", 48, F32), ("sv", P, F32), ("tw", 768, F32),
-                   ("mk", 24, F32), ("m1", CW, F32), ("sc", 12, F32), ("s1", 64 + 4 * CW, BF), ("s2", C + 512, BF),
-                   ("s3", 512, BF), ("zt", 512, BF), ("pm", 192, F32), ("sm", 4, F32), ("jk", 16, F32), ("ls", 12, F32),
-                   ("hm", C, BF), ("hq", 16, F32), ("hc", 4, F32), ("tt", C, F32), ("ys", H * P, F32)):
+                   ("eb", 520, BF), ("en", 520, BF), ("kt", 1536, BF), ("dd", 128, BF), ("m16", 128, BF), ("m16n", 256, BF),
+                   ("ta", 128, BF), ("tb", 128, BF), ("pi", 4, I32), ("pf", 8, F32), ("j48", 48, F32), ("j10", 16, F32),
+                   ("mk", 24, F32), ("m1", CW, F32), ("sc", 12, F32), ("sb", 12, F32), ("s1", 4 * CW, BF), ("s2", C + 512, BF),
+                   ("s3", 512, BF), ("lt", 512, BF), ("ha", 48, F32), ("hd", 4 * NP, F32), ("zt", 512, BF), ("pm", 176, F32),
+                   ("sm", 4, F32), ("jk", 16, F32), ("ls", 12, F32), ("lb", 12, F32), ("yw", P + C, F32), ("ys", H * P, F32)):
     SCRATCH[_n] = ("sbuf", [128, _w], _d)
 for _b in range(8):
     SCRATCH["ps%d" % _b] = ("psum", [128, 512], F32)
 
-SEMAPHORES = ["arr1", "arr2", "arr3", "sent", "ldP", "ldU", "ldX", "ldW", "gA", "gM", "gB", "gC", "z", "i0", "i1", "i2", "i3",
-              "i4", "i5", "i6", "i7", "i8", "ed", "a1", "a2", "a3", "a4", "ut", "en", "qP", "eqP", "eqN", "uq", "kq", "wq", "sS",
-              "sPen", "sM1", "sM2", "sM3", "z0", "z1", "z2", "z3", "sY", "vS", "t1", "q1", "pad", "t2", "q2", "t3", "q3", "ld",
-              "vL", "off", "pc", "ps", "sc", "zc", "zq", "vT", "oft", "tbC", "tbS", "aA", "yc", "out"]
+SEMAPHORES = ["arr1", "arr2", "arr3", "fw", "sent", "ldP", "ldU", "ldX", "ldW", "gA", "gM", "gB", "z", "i0", "i1", "i2", "i3",
+              "i4", "i6", "i8", "ed", "a1", "a2", "a3", "a4", "ut", "en", "qP", "eqP", "eqN", "uq", "kq", "wq", "pb", "sS",
+              "sPen", "sM1", "sM2", "sM3", "sM4", "sM5", "sM6", "z0", "z1", "z2", "z3", "sY", "vS", "t1", "q1", "t2", "q2",
+              "t3", "q3", "t4", "q4", "ld", "nm", "nC", "nS", "aB", "aL", "tL", "tH", "qL", "yw", "vB", "ofb", "aC", "aS",
+              "vL", "off", "pc", "ps", "zc", "zq", "oft", "tbC", "tbS", "aA", "yc", "out"]
 
 
 def rank_program(g, core, T, topo):
@@ -62,11 +70,14 @@ def rank_program(g, core, T, topo):
         return pe.matmul_mx(T["ps%d" % bank][:, 0:hi - lo], T[w + "c"][:, wlo:wlo + 128], T[w + "s"][:, wlo:wlo + 128],
                             T[x + "c"][:, lo:hi], T[x + "s"][:, lo:hi], start, stop)
 
-    def send(h, part, engines):
-        src, dst = T["p%d%s" % (h, part)][:, 0:P], T["q%d%s" % (h + 1, part)][:, 0:P]
+    def write(dst, src, sem, engines):
+        g.remote_dma(dst, src, S[sem], S.sent, pid, rid, sum(1 << e for e in engines))
+
+    def send(dst, dlo, src, part, sem, engines):
+        d, s = T[dst + part][:, dlo:dlo + P], T[src + part][:, 0:P]
         if part == "c":
-            src, dst = src.bitcast(dt.uint8), dst.bitcast(dt.uint8)
-        g.remote_dma(dst, src, S["arr%d" % (h + 1)], S.sent, pid, rid, sum(1 << e for e in engines))
+            d, s = d.bitcast(dt.uint8), s.bitcast(dt.uint8)
+        write(d, s, sem, engines)
 
     def pick_codes(dst, dlo, dhi, src, hi, off):
         return v.tensor_copy(T[dst + "c"][:, dlo:dhi].bitcast(dt.uint32), T[src + "c"][:, 0:hi].bitcast(dt.uint32).indirect(off))
@@ -79,15 +90,15 @@ def rank_program(g, core, T, topo):
     sy.dma_start(T.xt[:], T.x[:]).then_inc(S.ldX, 16)
     sy.dma_start(T.wt[:], T.w[:]).then_inc(S.ldW, 16)
     sy.wait_ge(S.yc, H - 1)
-    sy.wait_ge(S["arr%d" % H], 2 * ne)
+    sy.wait_ge(S.arr3, 2 * ne)
     sy.dma_start(T.y[:, 0:(H - 1) * P], T.ys[:, 0:(H - 1) * P]).then_inc(S.out, 16)
-    sy.wait_ge(S.pc, H)
-    sy.dma_start(T.pc[:], T["p%dc" % H][:, 0:P].bitcast(dt.uint8)).then_inc(S.out, 16)
-    sy.wait_ge(S.ps, H)
-    for k in range(4):
-        sy.dma_start(T.psc[4 * k:4 * k + 4, :], T["p%ds" % H][32 * k:32 * k + 4, 0:P]).then_inc(S.out, 16)
+    sy.wait_ge(S.pc, H - 1)
+    sy.dma_start(T.pc[:], T.p3c[:].bitcast(dt.uint8)).then_inc(S.out, 16)
     sy.wait_ge(S.yc, H)
     sy.dma_start(T.y[:, (H - 1) * P:H * P], T.ys[:, (H - 1) * P:H * P]).then_inc(S.out, 16)
+    sy.wait_ge(S.ps, H - 1)
+    for k in range(4):
+        sy.dma_start(T.psc[4 * k:4 * k + 4, :], T.p3s[32 * k:32 * k + 4, :]).then_inc(S.out, 16)
     sy.wait_ge(S.tbC, H + 1)
     sy.dma_start(T.oc[:], T.otc[:].bitcast(dt.uint8)).then_inc(S.out, 16)
     sy.wait_ge(S.tbS, H)
@@ -98,26 +109,33 @@ def rank_program(g, core, T, topo):
     fl = {"allow_small_or_imprecise_dtypes": True}
     g.iota(T.dd[:], [[1, 128]], 0, -1, **fl).then_inc(S.gA, 1)
     g.iota(T.pi[:, 0:1], [[1, 1]], 0, 1).then_inc(S.gM, 1)
-    g.iota(T.m16[:], [[0, C // 16], [1, 16]], 0, 0, **fl).then_inc(S.gM, 1)
+    g.iota(T.m16[:], [[0, 8], [1, 16]], 0, 0, **fl).then_inc(S.gM, 1)
     g.wait_ge(S.qP, 1)
-    send(0, "c", es[:ne // 2])
-    send(0, "s", es[ne // 2:])
+    send("q1", 0, "p0", "c", "arr1", es[:ne // 2])
+    send("q1", 0, "p0", "s", "arr1", es[ne // 2:])
     g.iota(T.j48[:], [[-1, 8 * NG]], 8 * NG - 1, 0, **fl).then_inc(S.gB, 1)
-    g.iota(T.sv[:], [[1, P]], P + C, 0, **fl).then_inc(S.gC, 1)
-    for h in range(H):
-        g.iota(T.tw[:, 256 * h + P:256 * h + 256], [[1, C]], P, 0, **fl).then_inc(S.gC, 1)
-    for h in range(1, H):
-        g.wait_ge(S.pc, h)
-        send(h, "c", es)
-        g.wait_ge(S.ps, h)
-        send(h, "s", es)
-    g.wait_ge(S.sent, ne * (2 * H - 1))
+    g.iota(T.j10[:, 0:NP], [[1, NP]], 1, 0, **fl).then_inc(S.gB, 1)
+    g.iota(T.m16n[:], [[0, 8], [1, 16], [0, 2]], -15, 0, **fl).then_inc(S.gB, 1)
+    g.wait_ge(S.arr1, ne)
+    send("r", 0, "q1", "c", "fw", es)
+    send("r", 0, "q1", "s", "fw", es)
+    g.wait_ge(S.nC, 1)
+    send("r", P, "na", "c", "fw", es)
+    g.wait_ge(S.nS, 1)
+    send("r", P, "na", "s", "fw", es)
+    g.wait_ge(S.ofb, 1)
+    write(T.lr[:, 0:NG], T.ofb[:, 0:NG], "arr2", es)
+    g.wait_ge(S.pc, 1)
+    send("q3", 0, "p2", "c", "arr3", es)
+    g.wait_ge(S.ps, 1)
+    send("q3", 0, "p2", "s", "arr3", es)
+    g.wait_ge(S.sent, 8 * ne)
 
     pr, pc = T.pf[:, 0:1], T.pf[:, 1:2]
     j6 = T.j48[:, 0:8 * NG:8]
     a.wait_ge(S.z, 1)
-    fills = ((T.s1[:, 67:64 + 4 * C:4], C, 1.0), (T.s1[:, 64 + 4 * C:64 + 4 * CW], 4 * (CW - C), 0.0), (T.s3[:], 512, 0.0),
-             (T.zt[:, 384:512], 128, 0.0), (T.pm[:, 0:17], 17, -BIG), (T.m1[:, 0:C], C, 1000.0))
+    fills = ((T.s1[:, 3:4 * C:4], C, 1.0), (T.s1[:, 4 * C:4 * CW], 4 * (CW - C), 0.0), (T.s3[:], 512, 0.0),
+             (T.zt[:, 384:512], 128, 0.0), (T.pm[:, 0:1], 1, -BIG), (T.m1[:, 0:C], C, 1000.0))
     for out, n, c in fills:
         a.activation(out, T.zero[:, 0:n], AF.Identity, bias=c).then_inc(S.a1, 1)
     a.wait_ge(S.ldU, 16)
@@ -126,25 +144,36 @@ def rank_program(g, core, T, topo):
     a.wait_ge(S.a2, 4)
     a.activation(T.ut[:, 640:1152], T.ut[:, 0:512], AF.Identity, scale=-1.0).then_inc(S.ut, 1)
     a.wait_ge(S.i4, 1)
-    a.activation(T.pf[:, 2:3], pc, AF.Identity, bias=2.0, scale=8.0).then_inc(S.a4, 1)
-    a.activation(T.pf[:, 3:4], pc, AF.Identity, bias=7.0, scale=8.0).then_inc(S.a4, 1)
-    a.activation(T.pf[:, 4:5], pr, AF.Identity, bias=-14.0).then_inc(S.a4, 1)
+    cols = ((2, pc, 8.0, 2.0), (3, pc, 8.0, 7.0), (4, pr, 1.0, -14.0), (5, pc, 16.0, float(C)), (6, pr, 1.0, 1.0),
+            (7, pr, 1.0, P - 14.0))
+    for k, src, scale, bias in cols:
+        a.activation(T.pf[:, k:k + 1], src, AF.Identity, bias=bias, scale=scale).then_inc(S.a4, 1)
     a.wait_ge(S.ed, 1)
     a.activation(T.en[:, 0:516], T.eb[:, 0:516], AF.Identity, scale=-0.5).then_inc(S.en, 1)
-    a.wait_ge(S.a4, 3)
-    a.wait_ge(S.gB, 1)
-    a.activation(T.sc[:, 1:12:2], j6, AF.Identity, bias=T.pf[:, 4:5], scale=2.0).then_inc(S.a3, 1)
-    a.wait_ge(S.i5, 1)
-    a.activation(T.hq[:], T.hm[:, 0:16], AF.Identity, bias=1.0, scale=-0.1875).then_inc(S.i7, 1)
-    a.wait_ge(S.i8, 1)
-    a.activation(T.mk[:, 8:14], T.mk[:, 0:6], AF.Identity, bias=-100.0, scale=105.0).then_inc(S.a3, 1)
-    a.activation(T.mk[:, 16:22], T.mk[:, 0:6], AF.Identity, bias=-100.0, scale=99.9375).then_inc(S.a3, 1)
-    a.wait_ge(S.a3, 3)
+    a.wait_ge(S.gM, 2)
     a.wait_ge(S.a1, len(fills))
+    a.wait_ge(S.a4, len(cols))
+    a.wait_ge(S.gB, 3)
+    fill2 = ((T.kt[:, 1026:1536:4], T.zero[:, 0:128], 1.0, 0.0), (T.kt[:, 1027:1536:4], T.zero[:, 0:128], 1.0, 0.0),
+             (T.lt[:, 3:512:4], T.zero[:, 0:128], 1.0, 0.0), (T.lt[P:128, 0:512:2], T.zero[P:128, 0:256], 1.0, 1.0),
+             (T.lt[P:128, 1:512:4], T.m16[P:128, :], 1.0, 0.0), (T.hd[:, 3:4 * NP:4], T.zero[:, 0:NP], 1.0, 0.0),
+             (T.s3[P:P + 1, 33:32 + 4 * NP:4], T.zero[P:P + 1, 0:NP], 1.0, 1.0),
+             (T.s3[0:1, 1:4 * NG:2], T.zero[0:1, 0:2 * NG], 1.0, 1.0),
+             (T.s3[P:P + 1, 32:32 + 4 * NP:4], T.j10[P:P + 1, 0:NP], 16.0, P - 16.0),
+             (T.sc[:, 1:12:2], j6, 2.0, T.pf[:, 4:5]), (T.sb[:, 1:12:2], j6, 2.0, T.pf[:, 4:5]),
+             (T.sb[:, 0:12:2], j6, 2.0, T.pf[:, 7:8]))
+    for out, src, scale, bias in fill2:
+        a.activation(out, src, AF.Identity, bias=bias, scale=scale).then_inc(S.a3, 1)
+    a.wait_ge(S.i8, 1)
+    a.activation(T.mk[:, 8:14], T.mk[:, 0:6], AF.Identity, bias=-100.0, scale=106.0).then_inc(S.a3, 1)
+    a.activation(T.mk[:, 16:22], T.mk[:, 0:6], AF.Identity, bias=-100.0, scale=99.9375).then_inc(S.a3, 1)
+    a.wait_ge(S.a3, 2 + len(fill2))
 
     v.memset(T.zero[:], 0.0).then_inc(S.z, 1)
     v.memset(T.pt[:, 4 * P:512], 0.0).then_inc(S.i0, 1)
     v.memset(T.eb[:], 0.0).then_inc(S.i1, 1)
+    v.wait_ge(S.z, 1)
+    quant("na", P, P + 128, T.zero[:]).then_inc(S.wq, 1)
     v.wait_ge(S.i1, 1)
     v.wait_ge(S.gA, 1)
     v.tensor_scalar(T.eb[:, 3:515:4], T.dd[:], 0.0, None, A.is_equal).then_inc(S.ed, 1)
@@ -156,8 +185,8 @@ def rank_program(g, core, T, topo):
     v.tensor_scalar(T.pi[:, 1:2], T.pi[:, 0:1], 15, None, A.bitwise_and).then_inc(S.i2, 1)
     v.tensor_scalar(T.pi[:, 2:3], T.pi[:, 0:1], 4, None, A.arith_shift_right).then_inc(S.i2, 1)
     v.tensor_scalar(T.tb[:], T.dd[:], 0.0, 512.0, A.is_equal, A.mult).then_inc(S.i2, 1)
-    v.tensor_scalar(T.kt[:, 2:512:4], T.dd[:], 0.0, -256.0, A.is_equal, A.mult).then_inc(S.i6, 1)
-    v.tensor_scalar(T.kt[:, 3:512:4], T.dd[:], 0.0, -512.0, A.is_equal, A.mult).then_inc(S.i6, 1)
+    for e, c, op in ((2, -256.0, A.is_equal), (3, -512.0, A.is_equal), (1024, float(G), A.is_equal), (1025, -1.0, A.is_gt)):
+        v.tensor_scalar(T.kt[:, e:e // 4 * 4 + 512:4], T.dd[:], 0.0, c, op, A.mult).then_inc(S.i6, 1)
     v.memset(T.s2[:, CW:C + 512], 0.0).then_inc(S.i6, 1)
     v.wait_ge(S.i2, 4)
     v.tensor_copy(T.pf[:, 0:2], T.pi[:, 1:3]).then_inc(S.i4, 1)
@@ -168,35 +197,32 @@ def rank_program(g, core, T, topo):
     v.wait_ge(S.i3, 1)
     v.tensor_scalar(T.kt[:, 1:512:4], T.kt[:, 0:512:4], -1.0, None, A.mult).then_inc(S.i6, 1)
     v.wait_ge(S.i4, 1)
-    v.tensor_scalar(T.hm[:], T.m16[:], pr, 4.0, A.is_gt, A.mult).then_inc(S.i5, 1)
     for e, c, op in ((512, float(G), A.is_equal), (513, -1.0, A.is_gt), (514, -float(G), A.is_equal), (515, -1.0, A.is_le)):
-        v.tensor_scalar(T.kt[:, e:1024:4], T.m16[:, 0:128], pr, c, op, A.mult).then_inc(S.i6, 1)
+        v.tensor_scalar(T.kt[:, e:1024:4], T.m16[:], pr, c, op, A.mult).then_inc(S.i6, 1)
     v.wait_ge(S.ldX, 16)
     quant("q1", P, P + C, T.xt[:]).then_inc(S.tbC, 1)
-    v.wait_ge(S.gB, 1)
-    v.wait_ge(S.a4, 3)
-    v.tensor_scalar(T.mk[:, 0:6], j6, T.pf[:, 3:4], None, A.is_equal).then_inc(S.i8, 1)
-    v.tensor_scalar(T.m1[:, C:CW], T.j48[:], T.pf[:, 2:3], 1000.0, A.is_ge, A.mult).then_inc(S.i6, 1)
     v.wait_ge(S.ut, 1)
     quant("uq", 0, 288, T.ut[:]).then_inc(S.uq, 1)
+    v.wait_ge(S.gB, 3)
+    v.wait_ge(S.a4, len(cols))
+    v.tensor_scalar(T.mk[:, 0:6], j6, T.pf[:, 3:4], None, A.is_equal).then_inc(S.i8, 1)
+    v.tensor_scalar(T.m1[:, C:CW], T.j48[:], T.pf[:, 2:3], 1000.0, A.is_ge, A.mult).then_inc(S.i6, 1)
     v.wait_ge(S.en, 1)
     for b in range(4):
         quant("eq", 512 + 128 * b, 640 + 128 * b, T.en[:, 3 - b:515 - b]).then_inc(S.eqN, 1)
-    v.wait_ge(S.i7, 1)
-    v.tensor_reduce(T.hc[:, 0:1], T.hq[:], AxisListType.X, A.mult).then_inc(S.i6, 1)
     v.wait_ge(S.ldW, 16)
     quant("wq", 0, 128, T.wt[:]).then_inc(S.wq, 1)
-    v.wait_ge(S.i6, 10)
-    v.wait_ge(S.a3, 3)
+    v.wait_ge(S.i6, 11)
+    quant("kq", 0, 256, T.kt[:, 0:1024]).then_inc(S.kq, 1)
+    v.wait_ge(S.a3, 2 + len(fill2))
     v.wait_ge(S.a1, len(fills))
-    quant("kq", 0, 256, T.kt[:]).then_inc(S.kq, 1)
+    quant("kq", 256, 384, T.kt[:, 1024:1536]).then_inc(S.kq, 1)
 
     for h in range(1, H + 1):
-        q, p = "q%d" % h, "p%d" % h
-        off, oft = T["off%d" % h][:, 0:NG], T["oft%d" % h][:, 0:C // 16]
+        q, p, nq = "q%d" % h, "p%d" % h, "na" if h == 1 else "nb"
+        off, nm, oft = T["off%d" % h][:, 0:NG], T["nm%d" % h][:, 0:NG], T["oft%d" % h][:, 0:NP]
         tdst, tlo = ("q%d" % (h + 1), P) if h < H else ("ot", 0)
-        tw0 = 256 * (h - 1)
-        top = T.pm[:, 16 + C:17 + C]
+        top = T.pm[:, C:C + 1]
         cw = CW if h == 1 else C
 
         pe.wait_ge(S.tbC, h)
@@ -205,85 +231,165 @@ def rank_program(g, core, T, topo):
         else:
             pe.wait_ge(S.tbS, h - 1)
         mm(1, "uq", C, q, P, P + C, True, False)
-        pe.wait_ge(S["arr%d" % h], ne if h == 1 else 2 * ne)
+        if h == 2:
+            pe.wait_ge(S.aC, 1)
+            pe.wait_ge(S.aS, 1)
+        else:
+            pe.wait_ge(S["arr%d" % h], ne if h == 1 else 2 * ne)
         mm(0, q, 0, q, P, P + C).then_inc(S.sS, 1)
         mm(1, q, 0, "uq", 0, C, False, True).then_inc(S.sPen, 1)
         if h == 1:
+            pe.wait_ge(S.wq, 2)
             pe.wait_ge(S.eqP, 4)
+        mm(3, "wq", 0, q, 0, P + C).then_inc(S.sY, 1)
         for b in range(4):
             mm(4 + b, "eq", 128 * b, q, 0, 128, True, False)
         if h == 1:
-            pe.wait_ge(S.kq, 1)
-        else:
-            pe.wait_ge(S.yc, h - 1)
+            pe.wait_ge(S.kq, 2)
         pe.wait_ge(S.q1, h)
         mm(2, "kq", 0, "c1", 0, cw).then_inc(S.sM1, 1)
         pe.wait_ge(S.q3, h)
+        mm(1, "kq", 128, "c3", 0, 128).then_inc(S.sM4, 1)
         mm(0, "kq", 128, "c3", 0, 128).then_inc(S.sM3, 1)
+        pe.wait_ge(S.yw, h)
         pe.wait_ge(S.q2, h)
-        mm(3, "kq", 128, "c2", 0, 128).then_inc(S.sM2, 1)
+        if h < H:
+            mm(3, "kq", 128, "c2", 0, 128).then_inc(S.sM2, 1)
+        pe.wait_ge(S.ld, h)
+        mm(0, "kq", 256, "c2", 0, 128).then_inc(S.sM5, 1)
+        if h == H:
+            mm(3, "kq", 128, "c2", 0, 128).then_inc(S.sM2, 1)
         if h == 1:
             pe.wait_ge(S.eqN, 4)
-            pe.wait_ge(S.wq, 1)
-        pe.wait_ge(S.pad, h)
-        pe.wait_ge(S.pc, h)
-        pe.wait_ge(S.ps, h)
+        if h == 2:
+            pe.wait_ge(S.pb, 1)
+        pe.wait_ge(S.nC, h)
+        pe.wait_ge(S.nS, h)
         for b in range(4):
-            mm(4 + b, "eq", 512 + 128 * b, p, 0, 128, False, True).then_inc(S["z%d" % b], 1)
-        mm(2, "wq", 0, p, 0, 128).then_inc(S.sY, 1)
+            mm(4 + b, "eq", 512 + 128 * b, nq, 0, 128, False, True).then_inc(S["z%d" % b], 1)
+        pe.wait_ge(S.qL, h)
+        pe.wait_ge(S.q4, h)
+        mm(1, "lq", 0, "c4", 0, 128).then_inc(S.sM6, 1)
 
+        if h == 2:
+            a.wait_ge(S.fw, 4 * ne)
+            a.wait_ge(S.arr2, ne)
+            pick_scales(q, 0, P, "r", 2 * P, T.lr[:, 0:NG]).then_inc(S.aS, 1)
         a.wait_ge(S.sPen, h)
-        a.activation(T.s1[:, 66:64 + 4 * C:4], T.ps1[:, 0:C], AF.Sign).then_inc(S.t1, 1)
+        a.activation(T.s1[:, 2:4 * C:4], T.ps1[:, 0:C], AF.Sign).then_inc(S.t1, 1)
         a.wait_ge(S.vS, h)
-        a.activation(T.s1[:, 1:64 + 4 * C:4], T.pm[:, 1:17 + C], AF.Sign, bias=top, scale=-1.0,
-                     accum_out=T.sm[:, 0:1]).then_inc(S.t1, 1)
-        a.activation(T.jk[:, 0:12], T.pm[:, 0:17 + C:16], AF.Sign, bias=top, scale=-1.0, accum_out=T.sm[:, 1:2]).then_inc(S.aA, 1)
+        a.activation(T.s1[:, 0:4 * C:4], T.pm[:, 0:C], AF.Sign, bias=top, scale=-1.0, accum_out=T.sm[:, 0:1]).then_inc(S.t1, 1)
+        a.activation(T.jk[:, 0:NP + 1], T.pm[:, 0:C + 1:16], AF.Sign, bias=top, scale=-1.0, accum_out=T.sm[:, 1:2]).then_inc(S.aA, 1)
         a.wait_ge(S.aA, h)
         a.activation(T.s3[:, 0:4 * NG:4], T.mk[:, 8:14], AF.Relu, bias=T.sm[:, 1:2]).then_inc(S.t3, 1)
         a.wait_ge(S.t1, 3 * h)
         a.activation(T.s3[:, 2:4 * NG:4], T.mk[:, 16:22], AF.Relu, bias=T.sm[:, 1:2], scale=T.sm[:, 0:1]).then_inc(S.t3, 1)
+        a.activation(T.sm[:, 2:3], T.sm[:, 1:2], AF.Identity, bias=T.sm[:, 0:1], scale=-16.0).then_inc(S.aB, 1)
+        a.activation(T.ha[:, 0:NP], T.j10[:, 0:NP], AF.Abs, bias=T.sm[:, 1:2], scale=-1.0).then_inc(S.aL, 1)
+        a.activation(T.sm[:, 3:4], T.sm[:, 1:2], AF.Identity, bias=T.pf[:, 5:6], scale=-16.0).then_inc(S.aL, 1)
+        a.wait_ge(S.sY, h)
+        if h > 1:
+            a.wait_ge(S.yc, h - 1)
+        a.activation(T.yw[:], T.ps3[:, 0:P + C], AF.Copy).then_inc(S.yw, 1)
+        a.wait_ge(S.aL, 4 * h - 2)
+        a.activation(T.ha[:, 16:16 + NP], T.ha[:, 0:NP], AF.Identity, bias=1.0, scale=-1.0).then_inc(S.aL, 1)
+        a.activation(T.ha[:, 32:32 + NP], T.ha[:, 0:NP], AF.Identity, bias=-1.0).then_inc(S.aL, 1)
+        a.wait_ge(S.aL, 4 * h)
+        a.wait_ge(S.aB, h)
+        for e, lo, col in ((0, 16, T.sm[:, 3:4]), (1, 32, T.sm[:, 2:3]), (2, 16, T.pf[:, 6:7])):
+            a.activation(T.hd[:, e:4 * NP:4], T.ha[:, lo:lo + NP], AF.Relu, scale=col).then_inc(S.tH, 1)
         a.wait_ge(S.sM3, h)
         a.activation(T.sc[:, 0:12:2], T.ps0[:, 0:NG], AF.Copy).then_inc(S.ld, 1)
-        a.wait_ge(S.off, h)
-        pick_scales(p, 0, P, q, 256, off).then_inc(S.ps, 1)
+        a.wait_ge(S.nm, h)
+        pick_scales(nq, 0, P, q, 256, nm).then_inc(S.nS, 1)
+        if h == 2:
+            a.wait_ge(S.off, h)
+            pick_scales(p, 0, P, q, 256, off).then_inc(S.ps, 1)
         for b in range(4):
             a.wait_ge(S["z%d" % b], h)
             a.activation(T.zt[:, b:384:4], T["ps%d" % (4 + b)][:, 0:P], AF.Copy).then_inc(S.zc, 1)
-        a.wait_ge(S.sY, h)
-        a.activation(T.ys[:, (h - 1) * P:h * P], T.ps2[:, 0:P], AF.Copy).then_inc(S.yc, 1)
+        a.wait_ge(S.off, h)
+        a.wait_ge(S.yw, h)
+        a.activation(T.ys[:, (h - 1) * P:h * P], T.yw[:].indirect(off), AF.Copy).then_inc(S.yc, 1)
+        if h == H:
+            pick_scales(p, 0, P, q, 256, off).then_inc(S.ps, 1)
         a.wait_ge(S.zq, h)
         a.wait_ge(S.oft, h)
         pick_scales(tdst, tlo, tlo + C, q, 384, oft).then_inc(S.tbS, 1)
 
+        if h == 2:
+            v.wait_ge(S.fw, 4 * ne)
+            v.wait_ge(S.arr2, ne)
+            pick_codes(q, 0, P, "r", 2 * P, T.lr[:, 0:NG]).then_inc(S.aC, 1)
         v.wait_ge(S.sS, h)
-        v.tensor_tensor_scan(T.pm[:, 17:17 + C], T.ps0[:, 0:C], T.zero[:, 0:C], -BIG, A.max, A.add).then_inc(S.vS, 1)
+        v.tensor_tensor_scan(T.pm[:, 1:C + 1], T.ps0[:, 0:C], T.zero[:, 0:C], -BIG, A.max, A.add).then_inc(S.vS, 1)
         v.wait_ge(S.vS, h)
-        v.tensor_scalar(T.s1[:, 64:64 + 4 * C:4], T.pm[:, 16:16 + C], top, None, A.is_lt).then_inc(S.t1, 1)
+        v.tensor_scalar(T.s1[:, 1:4 * C:4], T.pm[:, 1:C + 1], top, None, A.is_lt).then_inc(S.t1, 1)
         v.wait_ge(S.t1, 3 * h)
-        quant("c1", 0, cw, T.s1[:, 64:64 + 4 * cw]).then_inc(S.q1, 1)
+        quant("c1", 0, cw, T.s1[:, 0:4 * cw]).then_inc(S.q1, 1)
+        if h == 2:
+            quant("nb", P, P + 128, T.zero[:]).then_inc(S.pb, 1)
         v.wait_ge(S.t3, 2 * h)
         quant("c3", 0, 128, T.s3[:]).then_inc(S.q3, 1)
         v.wait_ge(S.sM1, h)
         v.tensor_tensor_scan(T.s2[:, 0:CW], T.ps2[:, 0:CW], T.m1[:], 0.0, A.max, A.min).then_inc(S.t2, 1)
+        v.wait_ge(S.sM4, h)
+        v.tensor_copy(nm, T.ps1[:, NG - 1::-1]).then_inc(S.nm, 1)
         v.wait_ge(S.t2, h)
         quant("c2", 0, 128, T.s2[:, C:C + 512]).then_inc(S.q2, 1)
-        quant(p, P, P + 128, T.zero[:]).then_inc(S.pad, 1)
-        v.wait_ge(S.ld, h)
-        v.wait_ge(S.sM2, h)
-        v.tensor_tensor_scan(T.ls[:], T.ps3[:, 0:12], T.sc[:], 0.0, A.min, A.max).then_inc(S.vL, 1)
-        v.wait_ge(S.vL, h)
-        v.tensor_copy(off, T.ls[:, 11::-2]).then_inc(S.off, 1)
-        v.wait_ge(S.off, h)
-        pick_codes(p, 0, P, q, 256, off).then_inc(S.pc, 1)
-        if h == 1:
-            v.wait_ge(S.gC, 1 + H)
-        v.tensor_copy(T.tw[:, tw0:tw0 + 256].indirect(off), T.sv[:]).then_inc(S.sc, 1)
-        v.wait_ge(S.sc, h)
-        v.tensor_tensor_scan(T.tt[:], T.hm[:], T.tw[:, tw0 + P:tw0 + 256], 0.0, A.mult, A.max).then_inc(S.vT, 1)
-        v.wait_ge(S.vT, h)
-        v.tensor_scalar(oft, T.tt[:, 15:C:16], T.hc[:, 0:1], None, A.mult).then_inc(S.oft, 1)
-        v.wait_ge(S.zc, 4 * h)
-        quant(q, 256, 384, T.zt[:]).then_inc(S.zq, 1)
+        v.wait_ge(S.aB, h)
+        v.tensor_scalar(T.lt[0:P, 1:512:4], T.m16n[0:P, 0:256:2], T.sm[0:P, 2:3], None, A.is_equal).then_inc(S.tL, 1)
+        v.wait_ge(S.nm, h)
+        pick_codes(nq, 0, P, q, 256, nm).then_inc(S.nC, 1)
+        v.tensor_scalar(T.lt[0:P, 0:512:2], T.m16n[0:P, :], T.sm[0:P, 2:3], None, A.is_equal).then_inc(S.tL, 1)
+
+        def far_scan():
+            v.wait_ge(S.sM2, h)
+            v.tensor_tensor_scan(T.lb[:], T.ps3[:, 0:12], T.sb[:], 0.0, A.min, A.max).then_inc(S.vB, 1)
+
+        def far_list():
+            v.wait_ge(S.vB, 1)
+            v.tensor_copy(T.ofb[:, 0:NG], T.lb[:, 11::-2]).then_inc(S.ofb, 1)
+
+        def panel_scan():
+            v.wait_ge(S.ld, h)
+            v.wait_ge(S.sM2, h)
+            v.tensor_tensor_scan(T.ls[:], T.ps3[:, 0:12], T.sc[:], 0.0, A.min, A.max).then_inc(S.vL, 1)
+
+        def panel_list():
+            v.wait_ge(S.vL, h)
+            v.tensor_copy(off, T.ls[:, 11::-2]).then_inc(S.off, 1)
+
+        def digits():
+            v.wait_ge(S.tH, 3 * h)
+            v.wait_ge(S.sM5, h)
+            v.tensor_scalar(T.s3[0:P, 32:32 + 4 * NP], T.hd[0:P, :], T.ps0[0:P, 0:1], 0.0, A.min, A.max).then_inc(S.t4, 1)
+
+        def quant_digits():
+            v.wait_ge(S.t4, h)
+            quant("c4", 0, 128, T.s3[:]).then_inc(S.q4, 1)
+
+        def quant_rows():
+            v.wait_ge(S.tL, 2 * h)
+            quant("lq", 0, 128, T.lt[:]).then_inc(S.qL, 1)
+
+        def panel():
+            v.wait_ge(S.off, h)
+            pick_codes(p, 0, P, q, 256, off).then_inc(S.pc, 1)
+
+        def table_list():
+            v.wait_ge(S.sM6, h)
+            v.tensor_copy(oft, T.ps1[:, 8:8 + NP]).then_inc(S.oft, 1)
+
+        def quant_z():
+            v.wait_ge(S.zc, 4 * h)
+            quant(q, 256, 384, T.zt[:]).then_inc(S.zq, 1)
+
+        order = ((far_scan, panel_scan, digits, far_list, quant_rows, quant_digits, panel_list, quant_z, table_list),
+                 (panel_scan, digits, panel_list, panel, quant_rows, quant_digits, quant_z, table_list),
+                 (digits, panel_scan, quant_rows, quant_digits, panel_list, panel, quant_z, table_list))
+        for step in order[h - 1]:
+            step()
         v.wait_ge(S.zq, h)
         v.wait_ge(S.oft, h)
         pick_codes(tdst, tlo, tlo + C, q, 384, oft).then_inc(S.tbC, 1)

from concourse.mybir import dt, AluOpType, AxisListType, ActivationFunctionType

P, C, G, H = 96, 160, 16, 3
X4, U8, BF, F32, U16, I32 = "float8_e4m3fn_x4", "uint8", "bfloat16", "float32", "uint16", "int32"
BIG = 1e29
NG = P // 16
NP = C // 16
CW = C + 8 * NG

SCRATCH = {}


def _mx(name, n):
    SCRATCH[name + "c"] = ("sbuf", [128, n], X4)
    SCRATCH[name + "s"] = ("sbuf", [128, n], U8)


_mx("p0", 128)
for _h in range(1, H + 1):
    _mx("q%d" % _h, 384)
    SCRATCH["off%d" % _h] = ("sbuf", [128, 8], U16)
    SCRATCH["nm%d" % _h] = ("sbuf", [128, 8], U16)
    SCRATCH["oft%d" % _h] = ("sbuf", [128, 16], U16)
SCRATCH["ofb"] = ("sbuf", [128, 8], U16)
SCRATCH["lr"] = ("sbuf", [128, 8], U16)
_mx("p2", P)
_mx("p3", P)
_mx("r", 2 * P)
_mx("ot", C)
_mx("na", 224)
_mx("nb", 224)
_mx("eq", 1024)
_mx("kq", 384)
_mx("uq", 288)
for _n in ("wq", "c2", "c3", "c4", "lq"):
    _mx(_n, 128)
_mx("c1", CW)
for _n, _w, _d in (("pt", 512, BF), ("xt", 640, BF), ("wt", 512, BF), ("ul", 8, BF), ("ut", 1152, BF), ("zero", 512, BF),
                   ("eb", 520, BF), ("en", 520, BF), ("kt", 1536, BF), ("dd", 128, BF), ("m16", 128, BF), ("m16n", 256, BF),
                   ("ta", 128, BF), ("tb", 128, BF), ("pi", 4, I32), ("pf", 8, F32), ("j48", 48, F32), ("j10", 16, F32),
                   ("mk", 24, F32), ("m1", CW, F32), ("sc", 12, F32), ("sb", 12, F32), ("s1", 4 * CW, BF), ("s2", C + 512, BF),
                   ("s3", 512, BF), ("lt", 512, BF), ("ha", 48, F32), ("hd", 4 * NP, F32), ("zt", 512, BF), ("pm", 176, F32),
                   ("sm", 4, F32), ("jk", 16, F32), ("ls", 12, F32), ("lb", 12, F32), ("yw", P + C, F32), ("ys", H * P, F32)):
    SCRATCH[_n] = ("sbuf", [128, _w], _d)
for _b in range(8):
    SCRATCH["ps%d" % _b] = ("psum", [128, 512], F32)

SEMAPHORES = ["arr1", "arr2", "arr3", "fw", "sent", "ldP", "ldU", "ldX", "ldW", "gA", "gM", "gB", "z", "i0", "i1", "i2", "i3",
              "i4", "i6", "i8", "ed", "a1", "a2", "a3", "a4", "ut", "en", "qP", "eqP", "eqN", "uq", "kq", "wq", "pb", "sS",
              "sPen", "sM1", "sM2", "sM3", "sM4", "sM5", "sM6", "z0", "z1", "z2", "z3", "sY", "vS", "t1", "q1", "t2", "q2",
              "t3", "q3", "t4", "q4", "ld", "nm", "nC", "nS", "aB", "aL", "tL", "tH", "qL", "yw", "vB", "ofb", "aC", "aS",
              "vL", "off", "pc", "ps", "zc", "zq", "oft", "tbC", "tbS", "aA", "yc", "out"]


def rank_program(g, core, T, topo):
    rank = T.rank_of(core)
    if rank is None:
        return
    A, AF = AluOpType, ActivationFunctionType
    v, a, pe, sy, S = g.vector, g.scalar, g.tensor, g.sync, T.sem
    nxt = T.cores[(rank + 1) % len(T.cores)]
    rid, pid, _ = topo.addr(nxt)
    es = topo.engines(core, nxt)
    ne = len(es)

    def quant(name, lo, hi, tile):
        return v.quantize_mx(T[name + "c"][:, lo:hi], T[name + "s"][:, lo:hi], tile)

    def mm(bank, w, wlo, x, lo, hi, start=True, stop=True):
        return pe.matmul_mx(T["ps%d" % bank][:, 0:hi - lo], T[w + "c"][:, wlo:wlo + 128], T[w + "s"][:, wlo:wlo + 128],
                            T[x + "c"][:, lo:hi], T[x + "s"][:, lo:hi], start, stop)

    def write(dst, src, sem, engines):
        g.remote_dma(dst, src, S[sem], S.sent, pid, rid, sum(1 << e for e in engines))

    def send(dst, dlo, src, part, sem, engines):
        d, s = T[dst + part][:, dlo:dlo + P], T[src + part][:, 0:P]
        if part == "c":
            d, s = d.bitcast(dt.uint8), s.bitcast(dt.uint8)
        write(d, s, sem, engines)

    def pick_codes(dst, dlo, dhi, src, hi, off):
        return v.tensor_copy(T[dst + "c"][:, dlo:dhi].bitcast(dt.uint32), T[src + "c"][:, 0:hi].bitcast(dt.uint32).indirect(off))

    def pick_scales(dst, dlo, dhi, src, hi, off):
        return a.activation(T[dst + "s"][:, dlo:dhi], T[src + "s"][:, 0:hi].indirect(off), AF.Copy)

    sy.dma_start(T.pt[:, 0:4 * P], T.pn[:]).then_inc(S.ldP, 16)
    sy.dma_start(T.ul[:, 0:4], T.u[:]).then_inc(S.ldU, 16)
    sy.dma_start(T.xt[:], T.x[:]).then_inc(S.ldX, 16)
    sy.dma_start(T.wt[:], T.w[:]).then_inc(S.ldW, 16)
    sy.wait_ge(S.yc, H - 1)
    sy.wait_ge(S.arr3, 2 * ne)
    sy.dma_start(T.y[:, 0:(H - 1) * P], T.ys[:, 0:(H - 1) * P]).then_inc(S.out, 16)
    sy.wait_ge(S.pc, H - 1)
    sy.dma_start(T.pc[:], T.p3c[:].bitcast(dt.uint8)).then_inc(S.out, 16)
    sy.wait_ge(S.yc, H)
    sy.dma_start(T.y[:, (H - 1) * P:H * P], T.ys[:, (H - 1) * P:H * P]).then_inc(S.out, 16)
    sy.wait_ge(S.ps, H - 1)
    for k in range(4):
        sy.dma_start(T.psc[4 * k:4 * k + 4, :], T.p3s[32 * k:32 * k + 4, :]).then_inc(S.out, 16)
    sy.wait_ge(S.tbC, H + 1)
    sy.dma_start(T.oc[:], T.otc[:].bitcast(dt.uint8)).then_inc(S.out, 16)
    sy.wait_ge(S.tbS, H)
    for k in range(2):
        sy.dma_start(T.osc[4 * k:4 * k + 4, :], T.ots[32 * k:32 * k + 4, :]).then_inc(S.out, 16)
    sy.wait_ge(S.out, 16 * 12)

    fl = {"allow_small_or_imprecise_dtypes": True}
    g.iota(T.dd[:], [[1, 128]], 0, -1, **fl).then_inc(S.gA, 1)
    g.iota(T.pi[:, 0:1], [[1, 1]], 0, 1).then_inc(S.gM, 1)
    g.iota(T.m16[:], [[0, 8], [1, 16]], 0, 0, **fl).then_inc(S.gM, 1)
    g.wait_ge(S.qP, 1)
    send("q1", 0, "p0", "c", "arr1", es[:ne // 2])
    send("q1", 0, "p0", "s", "arr1", es[ne // 2:])
    g.iota(T.j48[:], [[-1, 8 * NG]], 8 * NG - 1, 0, **fl).then_inc(S.gB, 1)
    g.iota(T.j10[:, 0:NP], [[1, NP]], 1, 0, **fl).then_inc(S.gB, 1)
    g.iota(T.m16n[:], [[0, 8], [1, 16], [0, 2]], -15, 0, **fl).then_inc(S.gB, 1)
    g.wait_ge(S.arr1, ne)
    send("r", 0, "q1", "c", "fw", es)
    send("r", 0, "q1", "s", "fw", es)
    g.wait_ge(S.nC, 1)
    send("r", P, "na", "c", "fw", es)
    g.wait_ge(S.nS, 1)
    send("r", P, "na", "s", "fw", es)
    g.wait_ge(S.ofb, 1)
    write(T.lr[:, 0:NG], T.ofb[:, 0:NG], "arr2", es)
    g.wait_ge(S.pc, 1)
    send("q3", 0, "p2", "c", "arr3", es)
    g.wait_ge(S.ps, 1)
    send("q3", 0, "p2", "s", "arr3", es)
    g.wait_ge(S.sent, 8 * ne)

    pr, pc = T.pf[:, 0:1], T.pf[:, 1:2]
    j6 = T.j48[:, 0:8 * NG:8]
    a.wait_ge(S.z, 1)
    fills = ((T.s1[:, 3:4 * C:4], C, 1.0), (T.s1[:, 4 * C:4 * CW], 4 * (CW - C), 0.0), (T.s3[:], 512, 0.0),
             (T.zt[:, 384:512], 128, 0.0), (T.pm[:, 0:1], 1, -BIG), (T.m1[:, 0:C], C, 1000.0))
    for out, n, c in fills:
        a.activation(out, T.zero[:, 0:n], AF.Identity, bias=c).then_inc(S.a1, 1)
    a.wait_ge(S.ldU, 16)
    for t in range(4):
        a.activation(T.ut[:, t:640:4], T.zero[:, 0:160], AF.Identity, bias=T.ul[:, t:t + 1]).then_inc(S.a2, 1)
    a.wait_ge(S.a2, 4)
    a.activation(T.ut[:, 640:1152], T.ut[:, 0:512], AF.Identity, scale=-1.0).then_inc(S.ut, 1)
    a.wait_ge(S.i4, 1)
    cols = ((2, pc, 8.0, 2.0), (3, pc, 8.0, 7.0), (4, pr, 1.0, -14.0), (5, pc, 16.0, float(C)), (6, pr, 1.0, 1.0),
            (7, pr, 1.0, P - 14.0))
    for k, src, scale, bias in cols:
        a.activation(T.pf[:, k:k + 1], src, AF.Identity, bias=bias, scale=scale).then_inc(S.a4, 1)
    a.wait_ge(S.ed, 1)
    a.activation(T.en[:, 0:516], T.eb[:, 0:516], AF.Identity, scale=-0.5).then_inc(S.en, 1)
    a.wait_ge(S.gM, 2)
    a.wait_ge(S.a1, len(fills))
    a.wait_ge(S.a4, len(cols))
    a.wait_ge(S.gB, 3)
    fill2 = ((T.kt[:, 1026:1536:4], T.zero[:, 0:128], 1.0, 0.0), (T.kt[:, 1027:1536:4], T.zero[:, 0:128], 1.0, 0.0),
             (T.lt[:, 3:512:4], T.zero[:, 0:128], 1.0, 0.0), (T.lt[P:128, 0:512:2], T.zero[P:128, 0:256], 1.0, 1.0),
             (T.lt[P:128, 1:512:4], T.m16[P:128, :], 1.0, 0.0), (T.hd[:, 3:4 * NP:4], T.zero[:, 0:NP], 1.0, 0.0),
             (T.s3[P:P + 1, 33:32 + 4 * NP:4], T.zero[P:P + 1, 0:NP], 1.0, 1.0),
             (T.s3[0:1, 1:4 * NG:2], T.zero[0:1, 0:2 * NG], 1.0, 1.0),
             (T.s3[P:P + 1, 32:32 + 4 * NP:4], T.j10[P:P + 1, 0:NP], 16.0, P - 16.0),
             (T.sc[:, 1:12:2], j6, 2.0, T.pf[:, 4:5]), (T.sb[:, 1:12:2], j6, 2.0, T.pf[:, 4:5]),
             (T.sb[:, 0:12:2], j6, 2.0, T.pf[:, 7:8]))
    for out, src, scale, bias in fill2:
        a.activation(out, src, AF.Identity, bias=bias, scale=scale).then_inc(S.a3, 1)
    a.wait_ge(S.i8, 1)
    a.activation(T.mk[:, 8:14], T.mk[:, 0:6], AF.Identity, bias=-100.0, scale=106.0).then_inc(S.a3, 1)
    a.activation(T.mk[:, 16:22], T.mk[:, 0:6], AF.Identity, bias=-100.0, scale=99.9375).then_inc(S.a3, 1)
    a.wait_ge(S.a3, 2 + len(fill2))

    v.memset(T.zero[:], 0.0).then_inc(S.z, 1)
    v.memset(T.pt[:, 4 * P:512], 0.0).then_inc(S.i0, 1)
    v.memset(T.eb[:], 0.0).then_inc(S.i1, 1)
    v.wait_ge(S.z, 1)
    quant("na", P, P + 128, T.zero[:]).then_inc(S.wq, 1)
    v.wait_ge(S.i1, 1)
    v.wait_ge(S.gA, 1)
    v.tensor_scalar(T.eb[:, 3:515:4], T.dd[:], 0.0, None, A.is_equal).then_inc(S.ed, 1)
    v.tensor_scalar(T.ta[:], T.dd[:], 0.0, -1024.0, A.is_gt, A.mult).then_inc(S.i2, 1)
    v.wait_ge(S.i0, 1)
    v.wait_ge(S.ldP, 16)
    quant("p0", 0, 128, T.pt[:]).then_inc(S.qP, 1)
    v.wait_ge(S.gM, 2)
    v.tensor_scalar(T.pi[:, 1:2], T.pi[:, 0:1], 15, None, A.bitwise_and).then_inc(S.i2, 1)
    v.tensor_scalar(T.pi[:, 2:3], T.pi[:, 0:1], 4, None, A.arith_shift_right).then_inc(S.i2, 1)
    v.tensor_scalar(T.tb[:], T.dd[:], 0.0, 512.0, A.is_equal, A.mult).then_inc(S.i2, 1)
    for e, c, op in ((2, -256.0, A.is_equal), (3, -512.0, A.is_equal), (1024, float(G), A.is_equal), (1025, -1.0, A.is_gt)):
        v.tensor_scalar(T.kt[:, e:e // 4 * 4 + 512:4], T.dd[:], 0.0, c, op, A.mult).then_inc(S.i6, 1)
    v.memset(T.s2[:, CW:C + 512], 0.0).then_inc(S.i6, 1)
    v.wait_ge(S.i2, 4)
    v.tensor_copy(T.pf[:, 0:2], T.pi[:, 1:3]).then_inc(S.i4, 1)
    v.tensor_tensor(T.kt[:, 0:512:4], T.ta[:], T.tb[:], A.add).then_inc(S.i3, 1)
    v.wait_ge(S.ed, 1)
    for b in range(4):
        quant("eq", 128 * b, 128 * b + 128, T.eb[:, 3 - b:515 - b]).then_inc(S.eqP, 1)
    v.wait_ge(S.i3, 1)
    v.tensor_scalar(T.kt[:, 1:512:4], T.kt[:, 0:512:4], -1.0, None, A.mult).then_inc(S.i6, 1)
    v.wait_ge(S.i4, 1)
    for e, c, op in ((512, float(G), A.is_equal), (513, -1.0, A.is_gt), (514, -float(G), A.is_equal), (515, -1.0, A.is_le)):
        v.tensor_scalar(T.kt[:, e:1024:4], T.m16[:], pr, c, op, A.mult).then_inc(S.i6, 1)
    v.wait_ge(S.ldX, 16)
    quant("q1", P, P + C, T.xt[:]).then_inc(S.tbC, 1)
    v.wait_ge(S.ut, 1)
    quant("uq", 0, 288, T.ut[:]).then_inc(S.uq, 1)
    v.wait_ge(S.gB, 3)
    v.wait_ge(S.a4, len(cols))
    v.tensor_scalar(T.mk[:, 0:6], j6, T.pf[:, 3:4], None, A.is_equal).then_inc(S.i8, 1)
    v.tensor_scalar(T.m1[:, C:CW], T.j48[:], T.pf[:, 2:3], 1000.0, A.is_ge, A.mult).then_inc(S.i6, 1)
    v.wait_ge(S.en, 1)
    for b in range(4):
        quant("eq", 512 + 128 * b, 640 + 128 * b, T.en[:, 3 - b:515 - b]).then_inc(S.eqN, 1)
    v.wait_ge(S.ldW, 16)
    quant("wq", 0, 128, T.wt[:]).then_inc(S.wq, 1)
    v.wait_ge(S.i6, 11)
    quant("kq", 0, 256, T.kt[:, 0:1024]).then_inc(S.kq, 1)
    v.wait_ge(S.a3, 2 + len(fill2))
    v.wait_ge(S.a1, len(fills))
    quant("kq", 256, 384, T.kt[:, 1024:1536]).then_inc(S.kq, 1)

    for h in range(1, H + 1):
        q, p, nq = "q%d" % h, "p%d" % h, "na" if h == 1 else "nb"
        off, nm, oft = T["off%d" % h][:, 0:NG], T["nm%d" % h][:, 0:NG], T["oft%d" % h][:, 0:NP]
        tdst, tlo = ("q%d" % (h + 1), P) if h < H else ("ot", 0)
        top = T.pm[:, C:C + 1]
        cw = CW if h == 1 else C

        pe.wait_ge(S.tbC, h)
        if h == 1:
            pe.wait_ge(S.uq, 1)
        else:
            pe.wait_ge(S.tbS, h - 1)
        mm(1, "uq", C, q, P, P + C, True, False)
        if h == 2:
            pe.wait_ge(S.aC, 1)
            pe.wait_ge(S.aS, 1)
        else:
            pe.wait_ge(S["arr%d" % h], ne if h == 1 else 2 * ne)
        mm(0, q, 0, q, P, P + C).then_inc(S.sS, 1)
        mm(1, q, 0, "uq", 0, C, False, True).then_inc(S.sPen, 1)
        if h == 1:
            pe.wait_ge(S.wq, 2)
            pe.wait_ge(S.eqP, 4)
        mm(3, "wq", 0, q, 0, P + C).then_inc(S.sY, 1)
        for b in range(4):
            mm(4 + b, "eq", 128 * b, q, 0, 128, True, False)
        if h == 1:
            pe.wait_ge(S.kq, 2)
        pe.wait_ge(S.q1, h)
        mm(2, "kq", 0, "c1", 0, cw).then_inc(S.sM1, 1)
        pe.wait_ge(S.q3, h)
        mm(1, "kq", 128, "c3", 0, 128).then_inc(S.sM4, 1)
        mm(0, "kq", 128, "c3", 0, 128).then_inc(S.sM3, 1)
        pe.wait_ge(S.yw, h)
        pe.wait_ge(S.q2, h)
        if h < H:
            mm(3, "kq", 128, "c2", 0, 128).then_inc(S.sM2, 1)
        pe.wait_ge(S.ld, h)
        mm(0, "kq", 256, "c2", 0, 128).then_inc(S.sM5, 1)
        if h == H:
            mm(3, "kq", 128, "c2", 0, 128).then_inc(S.sM2, 1)
        if h == 1:
            pe.wait_ge(S.eqN, 4)
        if h == 2:
            pe.wait_ge(S.pb, 1)
        pe.wait_ge(S.nC, h)
        pe.wait_ge(S.nS, h)
        for b in range(4):
            mm(4 + b, "eq", 512 + 128 * b, nq, 0, 128, False, True).then_inc(S["z%d" % b], 1)
        pe.wait_ge(S.qL, h)
        pe.wait_ge(S.q4, h)
        mm(1, "lq", 0, "c4", 0, 128).then_inc(S.sM6, 1)

        if h == 2:
            a.wait_ge(S.fw, 4 * ne)
            a.wait_ge(S.arr2, ne)
            pick_scales(q, 0, P, "r", 2 * P, T.lr[:, 0:NG]).then_inc(S.aS, 1)
        a.wait_ge(S.sPen, h)
        a.activation(T.s1[:, 2:4 * C:4], T.ps1[:, 0:C], AF.Sign).then_inc(S.t1, 1)
        a.wait_ge(S.vS, h)
        a.activation(T.s1[:, 0:4 * C:4], T.pm[:, 0:C], AF.Sign, bias=top, scale=-1.0, accum_out=T.sm[:, 0:1]).then_inc(S.t1, 1)
        a.activation(T.jk[:, 0:NP + 1], T.pm[:, 0:C + 1:16], AF.Sign, bias=top, scale=-1.0, accum_out=T.sm[:, 1:2]).then_inc(S.aA, 1)
        a.wait_ge(S.aA, h)
        a.activation(T.s3[:, 0:4 * NG:4], T.mk[:, 8:14], AF.Relu, bias=T.sm[:, 1:2]).then_inc(S.t3, 1)
        a.wait_ge(S.t1, 3 * h)
        a.activation(T.s3[:, 2:4 * NG:4], T.mk[:, 16:22], AF.Relu, bias=T.sm[:, 1:2], scale=T.sm[:, 0:1]).then_inc(S.t3, 1)
        a.activation(T.sm[:, 2:3], T.sm[:, 1:2], AF.Identity, bias=T.sm[:, 0:1], scale=-16.0).then_inc(S.aB, 1)
        a.activation(T.ha[:, 0:NP], T.j10[:, 0:NP], AF.Abs, bias=T.sm[:, 1:2], scale=-1.0).then_inc(S.aL, 1)
        a.activation(T.sm[:, 3:4], T.sm[:, 1:2], AF.Identity, bias=T.pf[:, 5:6], scale=-16.0).then_inc(S.aL, 1)
        a.wait_ge(S.sY, h)
        if h > 1:
            a.wait_ge(S.yc, h - 1)
        a.activation(T.yw[:], T.ps3[:, 0:P + C], AF.Copy).then_inc(S.yw, 1)
        a.wait_ge(S.aL, 4 * h - 2)
        a.activation(T.ha[:, 16:16 + NP], T.ha[:, 0:NP], AF.Identity, bias=1.0, scale=-1.0).then_inc(S.aL, 1)
        a.activation(T.ha[:, 32:32 + NP], T.ha[:, 0:NP], AF.Identity, bias=-1.0).then_inc(S.aL, 1)
        a.wait_ge(S.aL, 4 * h)
        a.wait_ge(S.aB, h)
        for e, lo, col in ((0, 16, T.sm[:, 3:4]), (1, 32, T.sm[:, 2:3]), (2, 16, T.pf[:, 6:7])):
            a.activation(T.hd[:, e:4 * NP:4], T.ha[:, lo:lo + NP], AF.Relu, scale=col).then_inc(S.tH, 1)
        a.wait_ge(S.sM3, h)
        a.activation(T.sc[:, 0:12:2], T.ps0[:, 0:NG], AF.Copy).then_inc(S.ld, 1)
        a.wait_ge(S.nm, h)
        pick_scales(nq, 0, P, q, 256, nm).then_inc(S.nS, 1)
        if h == 2:
            a.wait_ge(S.off, h)
            pick_scales(p, 0, P, q, 256, off).then_inc(S.ps, 1)
        for b in range(4):
            a.wait_ge(S["z%d" % b], h)
            a.activation(T.zt[:, b:384:4], T["ps%d" % (4 + b)][:, 0:P], AF.Copy).then_inc(S.zc, 1)
        a.wait_ge(S.off, h)
        a.wait_ge(S.yw, h)
        a.activation(T.ys[:, (h - 1) * P:h * P], T.yw[:].indirect(off), AF.Copy).then_inc(S.yc, 1)
        if h == H:
            pick_scales(p, 0, P, q, 256, off).then_inc(S.ps, 1)
        a.wait_ge(S.zq, h)
        a.wait_ge(S.oft, h)
        pick_scales(tdst, tlo, tlo + C, q, 384, oft).then_inc(S.tbS, 1)

        if h == 2:
            v.wait_ge(S.fw, 4 * ne)
            v.wait_ge(S.arr2, ne)
            pick_codes(q, 0, P, "r", 2 * P, T.lr[:, 0:NG]).then_inc(S.aC, 1)
        v.wait_ge(S.sS, h)
        v.tensor_tensor_scan(T.pm[:, 1:C + 1], T.ps0[:, 0:C], T.zero[:, 0:C], -BIG, A.max, A.add).then_inc(S.vS, 1)
        v.wait_ge(S.vS, h)
        v.tensor_scalar(T.s1[:, 1:4 * C:4], T.pm[:, 1:C + 1], top, None, A.is_lt).then_inc(S.t1, 1)
        v.wait_ge(S.t1, 3 * h)
        quant("c1", 0, cw, T.s1[:, 0:4 * cw]).then_inc(S.q1, 1)
        if h == 2:
            quant("nb", P, P + 128, T.zero[:]).then_inc(S.pb, 1)
        v.wait_ge(S.t3, 2 * h)
        quant("c3", 0, 128, T.s3[:]).then_inc(S.q3, 1)
        v.wait_ge(S.sM1, h)
        v.tensor_tensor_scan(T.s2[:, 0:CW], T.ps2[:, 0:CW], T.m1[:], 0.0, A.max, A.min).then_inc(S.t2, 1)
        v.wait_ge(S.sM4, h)
        v.tensor_copy(nm, T.ps1[:, NG - 1::-1]).then_inc(S.nm, 1)
        v.wait_ge(S.t2, h)
        quant("c2", 0, 128, T.s2[:, C:C + 512]).then_inc(S.q2, 1)
        v.wait_ge(S.aB, h)
        v.tensor_scalar(T.lt[0:P, 1:512:4], T.m16n[0:P, 0:256:2], T.sm[0:P, 2:3], None, A.is_equal).then_inc(S.tL, 1)
        v.wait_ge(S.nm, h)
        pick_codes(nq, 0, P, q, 256, nm).then_inc(S.nC, 1)
        v.tensor_scalar(T.lt[0:P, 0:512:2], T.m16n[0:P, :], T.sm[0:P, 2:3], None, A.is_equal).then_inc(S.tL, 1)

        def far_scan():
            v.wait_ge(S.sM2, h)
            v.tensor_tensor_scan(T.lb[:], T.ps3[:, 0:12], T.sb[:], 0.0, A.min, A.max).then_inc(S.vB, 1)

        def far_list():
            v.wait_ge(S.vB, 1)
            v.tensor_copy(T.ofb[:, 0:NG], T.lb[:, 11::-2]).then_inc(S.ofb, 1)

        def panel_scan():
            v.wait_ge(S.ld, h)
            v.wait_ge(S.sM2, h)
            v.tensor_tensor_scan(T.ls[:], T.ps3[:, 0:12], T.sc[:], 0.0, A.min, A.max).then_inc(S.vL, 1)

        def panel_list():
            v.wait_ge(S.vL, h)
            v.tensor_copy(off, T.ls[:, 11::-2]).then_inc(S.off, 1)

        def digits():
            v.wait_ge(S.tH, 3 * h)
            v.wait_ge(S.sM5, h)
            v.tensor_scalar(T.s3[0:P, 32:32 + 4 * NP], T.hd[0:P, :], T.ps0[0:P, 0:1], 0.0, A.min, A.max).then_inc(S.t4, 1)

        def quant_digits():
            v.wait_ge(S.t4, h)
            quant("c4", 0, 128, T.s3[:]).then_inc(S.q4, 1)

        def quant_rows():
            v.wait_ge(S.tL, 2 * h)
            quant("lq", 0, 128, T.lt[:]).then_inc(S.qL, 1)

        def panel():
            v.wait_ge(S.off, h)
            pick_codes(p, 0, P, q, 256, off).then_inc(S.pc, 1)

        def table_list():
            v.wait_ge(S.sM6, h)
            v.tensor_copy(oft, T.ps1[:, 8:8 + NP]).then_inc(S.oft, 1)

        def quant_z():
            v.wait_ge(S.zc, 4 * h)
            quant(q, 256, 384, T.zt[:]).then_inc(S.zq, 1)

        order = ((far_scan, panel_scan, digits, far_list, quant_rows, quant_digits, panel_list, quant_z, table_list),
                 (panel_scan, digits, panel_list, panel, quant_rows, quant_digits, quant_z, table_list),
                 (digits, panel_scan, quant_rows, quant_digits, panel_list, panel, quant_z, table_list))
        for step in order[h - 1]:
            step()
        v.wait_ge(S.zq, h)
        v.wait_ge(S.oft, h)
        pick_codes(tdst, tlo, tlo + C, q, 384, oft).then_inc(S.tbC, 1)

    a.wait_ge(S.tbS, H)
    for k in range(2, 4):
        a.dma_start(T.osc[4 * k:4 * k + 4, :], T.ots[32 * k:32 * k + 4, :]).then_inc(S.out, 16)
